import numpy as np
import ml_dtypes


def mxq(x, axis, fmt="e4m3"):
    dtype, down = {"e4m3": (ml_dtypes.float8_e4m3fn, 7), "e5m2": (ml_dtypes.float8_e5m2, 14)}[fmt]
    v = np.moveaxis(np.asarray(x, np.float32).astype(ml_dtypes.bfloat16).astype(np.float64), axis, -1)
    blocks = v.reshape(v.shape[:-1] + (-1, 32))
    amax = np.abs(blocks).max(-1, keepdims=True)
    byte = np.maximum(np.where(amax > 0, np.frexp(amax)[1] - 1 + 127, 0) - down, 1)
    scale = np.exp2(byte - 127.0)
    codes = (blocks / scale).astype(np.float32).astype(dtype).astype(np.float64)
    return np.moveaxis((codes * scale).reshape(v.shape), -1, axis)


WIDE = False


def mx_kscale(k):
    if not WIDE:
        return np.ones(k)
    levels = np.array([10, -10, 5, -5, 0])
    if k % 512:
        return np.exp2(np.random.permutation(np.resize(levels, k // 32))).repeat(32)
    a = np.empty((k // 512, 16))
    for p in range(k // 512):
        a[p, :8] = np.random.permutation(np.resize(levels, 8))
        for g in range(8):
            far = levels[np.abs(levels - a[p, g]) >= 10]
            a[p, g + 8] = far[np.random.randint(len(far))]
    return np.exp2(a.ravel()).repeat(32)


BF16 = ml_dtypes.bfloat16


def bf(x):
    return np.asarray(x, np.float32).astype(BF16)


def f64(x):
    return np.asarray(x).astype(np.float64)


E2M1 = np.array([0.0, 0.5, 1.0, 1.5, 2.0, 3.0, 4.0, 6.0, -0.0, -0.5, -1.0, -1.5, -2.0, -3.0, -4.0, -6.0])


def pack_weight(w, fmt):
    k, n = w.shape
    w = f64(bf(w)).reshape(k // 32, 32, n)
    amax = np.abs(w).max(1)
    if fmt == "e4m3":
        byte = np.frexp(amax)[1] - 1 + 127 - 7
    else:
        mant, ex = np.frexp(amax / 6.0)
        byte = np.where(mant > 0.5, ex, ex - 1) + 127
    byte = np.clip(np.where(amax > 0, byte, 1), 1, 254)
    scaled = (w * np.exp2(127.0 - byte)[:, None, :]).reshape(k, n).astype(np.float32)
    by_word = np.ascontiguousarray(scaled.reshape(k // 512, 128, 4, n).transpose(0, 1, 3, 2))
    if fmt == "e4m3":
        words = by_word.astype(ml_dtypes.float8_e4m3fn).view(np.uint8)
    else:
        c = by_word.astype(ml_dtypes.float4_e2m1fn).view(np.uint8) & 0xF
        words = c[..., 0::2] | (c[..., 1::2] << 4)
    return np.ascontiguousarray(words), np.ascontiguousarray(byte.astype(np.uint8).reshape(k // 512, 16, n))


def unpack_weight(words, scales, fmt):
    g, p, n, _ = words.shape
    if fmt == "e4m3":
        vals = np.ascontiguousarray(words).view(ml_dtypes.float8_e4m3fn).astype(np.float64)
    else:
        nib = np.empty((g, p, n, 4), np.uint8)
        nib[..., 0::2] = words & 0xF
        nib[..., 1::2] = words >> 4
        vals = E2M1[nib]
    vals = vals * np.repeat(np.exp2(scales.astype(np.float64) - 127.0), 8, axis=1)[..., None]
    return vals.transpose(0, 1, 3, 2).reshape(g * 512, n)
def pack4(w):
    words, scales = pack_weight(w, "e2m1")
    return words.reshape(words.shape[0], 128, -1), scales


def unpack4(words, scales):
    return unpack_weight(words.reshape(words.shape[0], 128, -1, 2), scales, "e2m1")


E4M3FN = np.array([(-1.0 if i & 128 else 1.0) * ((1.0 + (i & 7) / 8.0) * 2.0 ** (((i >> 3) & 15) - 7) if i & 120 else (i & 7) * 2.0 ** -9) for i in range(256)])


def e4m3fn_bytes(y):
    return np.clip(np.asarray(y, np.float64), -448.0, 448.0).astype(np.float32).astype(ml_dtypes.float8_e4m3fn).view(np.uint8)


def e4m3fn_values(b):
    return E4M3FN[b]


T, A, L, B = 1024, 1024, 2048, 128


def setup_inputs():
    s, t = mx_kscale(A), mx_kscale(L)
    C = np.random.standard_normal((T, A)) * s
    C_scale = (np.abs(C).reshape(T, A // B, B).max(axis=2) / 448).astype(np.float32)
    C_bytes = e4m3fn_bytes(C / np.repeat(f64(C_scale), B, axis=1))
    G_words, G_scales = pack4(np.random.standard_normal((A, L)) / np.sqrt(A) / s[:, None] * t)
    R = np.random.standard_normal((A, L)) / np.sqrt(L) / t
    R_scale = (np.abs(R).reshape(A // B, B, L // B, B).max(axis=(1, 3)) / 448).astype(np.float32)
    R_bytes = e4m3fn_bytes(R / np.repeat(np.repeat(f64(R_scale), B, axis=0), B, axis=1))
    return {"C_bytes": C_bytes, "C_scale": C_scale,
            "G_words": G_words, "G_scales": G_scales,
            "slopes": bf(np.random.standard_normal((T, L)) * t),
            "R_bytes": R_bytes, "R_scale": R_scale,
            "gain": bf(np.random.uniform(0.4, 0.8, A)),
            "leak": bf(np.random.uniform(0.6, 0.95, A)),
            "prev": bf(np.random.standard_normal((T, A)))}


def reference(C_bytes, C_scale, G_words, G_scales, slopes, R_bytes, R_scale, gain, leak, prev):
    C = e4m3fn_values(C_bytes) * np.repeat(f64(C_scale), B, axis=1)
    R = e4m3fn_values(R_bytes) * np.repeat(np.repeat(f64(R_scale), B, axis=0), B, axis=1)
    mirror = mxq(C, 1, "e4m3") @ unpack4(G_words, G_scales)
    full = f64(slopes) + mirror
    e = mxq(full, 1, "e4m3") @ mxq(R, 1, "e4m3").T
    return f64(leak) * f64(prev) + f64(gain) * e

@@ -1,0 +1,281 @@
+from contextlib import ExitStack
+
+import concourse.mybir as mybir
+from concourse.masks import make_identity
+
+T, A, L = 1024, 1024, 2048
+P = 128
+FLOPS = 2 * T * A * L * 2
+
+F32 = mybir.dt.float32
+BF16 = mybir.dt.bfloat16
+I32 = mybir.dt.int32
+U32 = mybir.dt.uint32
+U8 = mybir.dt.uint8
+FP8 = mybir.dt.float8_e4m3fn
+FP8X4 = mybir.dt.float8_e4m3fn_x4
+FP4X4 = mybir.dt.float4_e2m1fn_x4
+MULT = mybir.AluOpType.mult
+ADD = mybir.AluOpType.add
+COPY = mybir.ActivationFunctionType.Copy
+
+NT = T // P
+NR = A // P
+GA = A // 512
+GL = L // 512
+NL = L // 512
+NA = A // 512
+
+
+def tile_leaky_slope_reconstructor_d6_kernel(
+    tc, C_bytes, C_scale, G_words, G_scales, slopes, R_bytes, R_scale, gain, leak, prev, out
+):
+    nc = tc.nc
+    with ExitStack() as ctx:
+        keep = ctx.enter_context(tc.tile_pool(name="keep", bufs=1))
+        work = ctx.enter_context(tc.tile_pool(name="work", bufs=3))
+        psum = ctx.enter_context(tc.psum_pool(name="psum", bufs=1))
+
+        c_raw = keep.tile([P, NT, A], U8, align_bytes=64)
+        c_sc = keep.tile([P, NT, A // P], F32, align_bytes=64)
+        g_words = keep.tile([P, GA, 2 * L], U8, align_bytes=64)
+        g_sc = keep.tile([P, GA, L], U8, align_bytes=64)
+        r_raw = keep.tile([P, NR, L], U8, align_bytes=64)
+        r_sc = keep.tile([P, NR * (L // P)], F32, align_bytes=64)
+        s_sb = keep.tile([P, NT, L], BF16, align_bytes=64)
+        prev_sb = keep.tile([P, NT, A], BF16, align_bytes=64)
+        gain_sb = keep.tile([P, A], BF16, align_bytes=64)
+        leak_sb = keep.tile([P, A], BF16, align_bytes=64)
+        ident = keep.tile([P, P], F32, align_bytes=64)
+        c_codes = keep.tile([P, NT, GA * P], U32, align_bytes=64)
+        c_planes = keep.tile([P, NT, GA * P], U8, align_bytes=64)
+        r_codes = keep.tile([P, GL, A], U32, align_bytes=64)
+        r_planes = keep.tile([P, GL, A], U8, align_bytes=64)
+        f_codes = keep.tile([P, NT, GL * P], U32, align_bytes=64)
+        f_planes = keep.tile([P, NT, GL * P], U8, align_bytes=64)
+
+        c_v = C_bytes.rearrange("(p i) k -> p i k", i=NT)
+        s_v = slopes.rearrange("(p i) l -> p i l", i=NT)
+        p_v = prev.rearrange("(p i) a -> p i a", i=NT)
+        o_v = out.rearrange("(p i) a -> p i a", i=NT)
+        r_v = R_bytes.rearrange("(i p) l -> p i l", p=P)
+
+        make_identity(nc, ident[:])
+        nc.vector.memset(g_sc[:].rearrange("p g n -> p (g n)").bitcast(I32), 0)
+
+        nc.scalar.dma_start(out=r_sc[:], in_=R_scale.rearrange("i j -> (i j)").partition_broadcast(P))
+        for q in range(4):
+            nc.scalar.dma_start(
+                out=g_sc[32 * q : 32 * q + 4, :, :].bitcast(I32),
+                in_=G_scales[:, 4 * q : 4 * q + 4, :].rearrange("g q n -> q g n").bitcast(I32),
+            )
+        nc.sync.dma_start(out=c_sc[:], in_=C_scale.rearrange("(p i) j -> p i j", i=NT))
+        nc.sync.dma_start(out=c_raw[:, 0:2, :], in_=c_v[:, 0:2, :])
+        nc.sync.dma_start(out=g_words[:, :, 0:1024].bitcast(I32), in_=G_words.rearrange("g p n -> p g n")[:, :, 0:1024].bitcast(I32))
+        nc.sync.dma_start(out=s_sb[:, 0, :], in_=s_v[:, 0, :])
+        nc.sync.dma_start(out=g_words[:, :, 1024:2048].bitcast(I32), in_=G_words.rearrange("g p n -> p g n")[:, :, 1024:2048].bitcast(I32))
+        nc.sync.dma_start(out=g_words[:, :, 2048:3072].bitcast(I32), in_=G_words.rearrange("g p n -> p g n")[:, :, 2048:3072].bitcast(I32))
+        nc.sync.dma_start(out=g_words[:, :, 3072:4096].bitcast(I32), in_=G_words.rearrange("g p n -> p g n")[:, :, 3072:4096].bitcast(I32))
+        nc.sync.dma_start(out=r_raw[:, 0:1, :], in_=r_v[:, 0:1, :])
+        nc.sync.dma_start(out=s_sb[:, 1, :], in_=s_v[:, 1, :])
+        nc.sync.dma_start(out=r_raw[:, 1:2, :], in_=r_v[:, 1:2, :])
+        nc.sync.dma_start(out=c_raw[:, 2:5, :], in_=c_v[:, 2:5, :])
+        nc.sync.dma_start(out=r_raw[:, 2:3, :], in_=r_v[:, 2:3, :])
+        nc.sync.dma_start(out=s_sb[:, 2, :], in_=s_v[:, 2, :])
+        nc.sync.dma_start(out=leak_sb[:], in_=leak.partition_broadcast(P))
+        nc.sync.dma_start(out=prev_sb[:, 0:2, :], in_=p_v[:, 0:2, :])
+        nc.sync.dma_start(out=r_raw[:, 3:4, :], in_=r_v[:, 3:4, :])
+        nc.sync.dma_start(out=s_sb[:, 3, :], in_=s_v[:, 3, :])
+        nc.sync.dma_start(out=r_raw[:, 4:6, :], in_=r_v[:, 4:6, :])
+        nc.sync.dma_start(out=prev_sb[:, 2:4, :], in_=p_v[:, 2:4, :])
+        nc.sync.dma_start(out=c_raw[:, 5:8, :], in_=c_v[:, 5:8, :])
+        nc.sync.dma_start(out=s_sb[:, 4, :], in_=s_v[:, 4, :])
+        nc.sync.dma_start(out=r_raw[:, 6:8, :], in_=r_v[:, 6:8, :])
+        nc.sync.dma_start(out=s_sb[:, 5, :], in_=s_v[:, 5, :])
+        nc.sync.dma_start(out=gain_sb[:], in_=gain.partition_broadcast(P))
+        nc.sync.dma_start(out=prev_sb[:, 4:8, :], in_=p_v[:, 4:8, :])
+        nc.sync.dma_start(out=s_sb[:, 6, :], in_=s_v[:, 6, :])
+        nc.sync.dma_start(out=s_sb[:, 7, :], in_=s_v[:, 7, :])
+        def widen(dst, raw, scale, on_vector):
+            if on_vector:
+                nc.vector.tensor_scalar(out=dst, in0=raw.bitcast(FP8), scalar1=scale, scalar2=None, op0=MULT)
+            else:
+                nc.scalar.activation(out=dst, in_=raw.bitcast(FP8), func=COPY, scale=scale)
+
+        def turn(values, groups, dst):
+            words = values.bitcast(F32)
+            for g0 in range(0, groups, 2):
+                bank = psum.tile([P, 2, 2, P], F32, tag="turn", bufs=3, name="bank")
+                for g in range(2):
+                    for u in range(2):
+                        w0 = 256 * (g0 + g) + u
+                        nc.tensor.transpose(bank[:, g, u, :], words[:, w0 : w0 + 255 : 2], ident[:])
+                nc.scalar.copy(
+                    out=dst[:, g0 : g0 + 2, :, :].bitcast(F32),
+                    in_=bank[:].rearrange("p g u r -> p g r u"),
+                )
+
+        c_four = {}
+        c_wide = {}
+
+        def widen_c(i, on_vector):
+            c_wide[i] = work.tile([P, A], BF16, tag="c_wide", bufs=2, align_bytes=64, name="c_w")
+            for j in range(A // P):
+                k = slice(P * j, P * (j + 1))
+                widen(c_wide[i][:, k], c_raw[:, i, k], c_sc[:, i, j : j + 1], on_vector)
+
+        def turn_c(i):
+            c_four[i] = work.tile([P, GA, P, 4], BF16, tag="c_four", bufs=2, align_bytes=64, name="c_f")
+            turn(c_wide[i][:], GA, c_four[i])
+
+        def quant_c(i):
+            nc.vector.quantize_mx(
+                out=c_codes[:, i, :].bitcast(FP8X4),
+                scales=c_planes[:, i, :],
+                in_=c_four[i][:].rearrange("p g r j -> p (g r j)"),
+            )
+
+        r_four = {}
+        r_wide = {}
+
+        def widen_r(i, on_vector):
+            r_wide[i] = work.tile([P, L], BF16, tag="r_wide", bufs=3, align_bytes=64, name="r_w")
+            for j in range(L // P):
+                k = slice(P * j, P * (j + 1))
+                s = i * (L // P) + j
+                widen(r_wide[i][:, k], r_raw[:, i, k], r_sc[:, s : s + 1], on_vector)
+
+        def turn_r(i):
+            r_four[i] = work.tile([P, GL, P, 4], BF16, tag="r_four", bufs=3, align_bytes=64, name="r_f")
+            turn(r_wide[i][:], GL, r_four[i])
+
+        def quant_r(i):
+            cols = slice(P * i, P * (i + 1))
+            for g in range(GL):
+                nc.vector.quantize_mx(
+                    out=r_codes[:, g, cols].bitcast(FP8X4),
+                    scales=r_planes[:, g, cols],
+                    in_=r_four[i][:, g, :, :].rearrange("p r j -> p (r j)"),
+                )
+
+        full = {}
+        f_four = {}
+
+        def mirror(i):
+            full[i] = work.tile([P, GL, 2, P, 2], BF16, tag="full", bufs=2, align_bytes=64, name="full_t")
+            for n in range(NL):
+                acc = psum.tile([P, 512], F32, tag="acc", bufs=3, name="acc")
+                for g in range(GA):
+                    nc.tensor.matmul_mx(
+                        out=acc[:],
+                        lhsT=c_codes[:, i, P * g : P * (g + 1)].bitcast(FP8X4),
+                        lhsT_scale=c_planes[:, i, P * g : P * (g + 1)],
+                        rhs=g_words[:, g, 1024 * n : 1024 * (n + 1)].bitcast(FP4X4),
+                        rhs_scale=g_sc[:, g, 512 * n : 512 * (n + 1)],
+                        start=(g == 0),
+                        stop=(g == GA - 1),
+                    )
+                nc.vector.tensor_tensor(
+                    out=full[i][:, n, :, :, :],
+                    in0=acc[:].rearrange("p (w u e) -> p u w e", u=2, e=2),
+                    in1=s_sb[:, i, 512 * n : 512 * (n + 1)].rearrange("p (w u e) -> p u w e", u=2, e=2),
+                    op=ADD,
+                )
+
+        def turn_f(i):
+            f_four[i] = work.tile([P, GL, P, 4], BF16, tag="f_four", bufs=2, align_bytes=64, name="f_f")
+            words = full[i][:].rearrange("p g u w e -> p (g u w e)").bitcast(F32)
+            for g0 in range(0, GL, 2):
+                bank = psum.tile([P, 2, 2, P], F32, tag="turn", bufs=3, name="bank")
+                for g in range(2):
+                    for u in range(2):
+                        w0 = P * (2 * (g0 + g) + u)
+                        nc.tensor.transpose(bank[:, g, u, :], words[:, w0 : w0 + P], ident[:])
+                nc.scalar.copy(
+                    out=f_four[i][:, g0 : g0 + 2, :, :].bitcast(F32),
+                    in_=bank[:].rearrange("p g u r -> p g r u"),
+                )
+
+        def quant_f(i):
+            nc.vector.quantize_mx(
+                out=f_codes[:, i, :].bitcast(FP8X4),
+                scales=f_planes[:, i, :],
+                in_=f_four[i][:].rearrange("p g r j -> p (g r j)"),
+            )
+
+        left = {}
+
+        def leaky(i):
+            left[i] = work.tile([P, A], F32, tag="left", bufs=8, align_bytes=64, name="left_t")
+            nc.vector.tensor_tensor(out=left[i][:], in0=prev_sb[:, i, :], in1=leak_sb[:], op=MULT)
+
+        def react(i, c):
+            cols = slice(512 * c, 512 * (c + 1))
+            acc2 = psum.tile([P, 512], F32, tag="acc2", bufs=2, name="acc2")
+            for g in range(GL):
+                nc.tensor.matmul_mx(
+                    out=acc2[:],
+                    lhsT=f_codes[:, i, P * g : P * (g + 1)].bitcast(FP8X4),
+                    lhsT_scale=f_planes[:, i, P * g : P * (g + 1)],
+                    rhs=r_codes[:, g, cols].bitcast(FP8X4),
+                    rhs_scale=r_planes[:, g, cols],
+                    start=(g == 0),
+                    stop=(g == GL - 1),
+                )
+            gained[i, c] = work.tile([P, 512], F32, tag="gained", bufs=4, align_bytes=64, name="gained_t")
+            nc.vector.tensor_tensor(out=gained[i, c][:], in0=acc2[:], in1=gain_sb[:, cols], op=MULT)
+
+        gained = {}
+
+        def finish(i, c):
+            cols = slice(512 * c, 512 * (c + 1))
+            nc.vector.tensor_tensor(out=left[i][:, cols], in0=gained[i, c][:], in1=left[i][:, cols], op=ADD)
+            nc.sync.dma_start(out=o_v[:, i, cols], in_=left[i][:, cols])
+
+
+        V_R = (0, 1)
+        TURN_R = [[0], [1, 2], [3], [4], [5], [6], [7], []]
+        REACT = [[], [], [], [], [(0, 0),(1, 0),(2, 0)], [(3, 0),(4, 0)], [(5, 0)], [(6, 0)], [(0, 1),(1, 1),(2, 1),(3, 1),(4, 1),(5, 1),(6, 1), (7, 0), (7, 1)]]
+        LEAKY = [[], [0], [1], [2], [3, 4], [5], [6], [7]]
+        if True:
+            widen_c(0, True)
+            widen_c(1, False)
+            turn_c(0)
+            quant_c(0)
+            turn_c(1)
+            quant_c(1)
+            widen_c(2, False)
+            pend_q = []
+            pend_f = []
+            for i in TURN_R[0]:
+                widen_r(i, i in V_R)
+            for s in range(NT):
+                mirror(s)
+                for i, c in REACT[s]:
+                    react(i, c)
+                if s + 2 < NT:
+                    turn_c(s + 2)
+                for i in TURN_R[s]:
+                    turn_r(i)
+                turn_f(s)
+                if s + 3 < NT:
+                    widen_c(s + 3, False)
+                if s + 1 < NT:
+                    for i in TURN_R[s + 1]:
+                        widen_r(i, i in V_R)
+                for i, c in REACT[s]:
+                    finish(i, c)
+                if s + 2 < NT:
+                    quant_c(s + 2)
+                for i in LEAKY[s]:
+                    leaky(i)
+                for i in TURN_R[s]:
+                    quant_r(i)
+                quant_f(s)
+            last = None
+            for i, c in REACT[NT]:
+                react(i, c)
+                if last:
+                    finish(*last)
+                last = (i, c)
+            finish(*last)

@@ -20,11 +20,16 @@ ADD = mybir.AluOpType.add
 COPY = mybir.ActivationFunctionType.Copy
 
 NT = T // P
-NR = A // P
 GA = A // 512
 GL = L // 512
 NL = L // 512
-NA = A // 512
+SPAN = 1024
+QW = 256
+NQ = A // QW
+NPAIR = NT // 2
+NRU = (A // P) * (L // SPAN)
+HEAD_C = 2
+HEAD_R = 2
 
 
 def tile_leaky_slope_reconstructor_d6_kernel(
@@ -33,249 +38,306 @@ def tile_leaky_slope_reconstructor_d6_kernel(
     nc = tc.nc
     with ExitStack() as ctx:
         keep = ctx.enter_context(tc.tile_pool(name="keep", bufs=1))
-        work = ctx.enter_context(tc.tile_pool(name="work", bufs=3))
         psum = ctx.enter_context(tc.psum_pool(name="psum", bufs=1))
+        ctx.enter_context(tc.manual_schedule())
 
-        c_raw = keep.tile([P, NT, A], U8, align_bytes=64)
-        c_sc = keep.tile([P, NT, A // P], F32, align_bytes=64)
-        g_words = keep.tile([P, GA, 2 * L], U8, align_bytes=64)
-        g_sc = keep.tile([P, GA, L], U8, align_bytes=64)
-        r_raw = keep.tile([P, NR, L], U8, align_bytes=64)
-        r_sc = keep.tile([P, NR * (L // P)], F32, align_bytes=64)
-        s_sb = keep.tile([P, NT, L], BF16, align_bytes=64)
-        prev_sb = keep.tile([P, NT, A], BF16, align_bytes=64)
-        gain_sb = keep.tile([P, A], BF16, align_bytes=64)
-        leak_sb = keep.tile([P, A], BF16, align_bytes=64)
-        ident = keep.tile([P, P], F32, align_bytes=64)
-        c_codes = keep.tile([P, NT, GA * P], U32, align_bytes=64)
-        c_planes = keep.tile([P, NT, GA * P], U8, align_bytes=64)
-        r_codes = keep.tile([P, GL, A], U32, align_bytes=64)
-        r_planes = keep.tile([P, GL, A], U8, align_bytes=64)
-        f_codes = keep.tile([P, NT, GL * P], U32, align_bytes=64)
-        f_planes = keep.tile([P, NT, GL * P], U8, align_bytes=64)
+        def tiles(name, count, shape, dtype):
+            return [keep.tile(shape, dtype, align_bytes=64, name="%s%d" % (name, k)) for k in range(count)]
+
+        c_raw = tiles("c_raw", 3, [P, 3, A], U8)
+        c_sc = tiles("c_sc", 1, [P, NT, A // P], F32)[0]
+        g_words = tiles("g_words", NL, [P, GA, 1024], U8)
+        g_sc = tiles("g_sc", 1, [P, GA, L], U8)[0]
+        r_raw = tiles("r_raw", 2 * NQ, [P, 2, SPAN], U8)
+        r_sc = tiles("r_sc", 1, [P, (A // P) * (L // P)], F32)[0]
+        s_sb = tiles("s_sb", NT, [P, L], BF16)
+        prev_sb = tiles("prev_sb", 4, [P, NT // 2, A // 2], BF16)
+        gain_sb = tiles("gain_sb", 1, [P, A], BF16)[0]
+        leak_sb = tiles("leak_sb", 1, [P, A], BF16)[0]
+        ident = tiles("ident", 1, [P, P], F32)[0]
+        wide = tiles("wide", 8, [P, SPAN], BF16)
+        c_four = tiles("c_four", 2, [P, GA, P, 4], BF16)
+        c_codes = tiles("c_codes", 3, [P, GA * P], U32)
+        c_planes = tiles("c_planes", 3, [P, GA * P], U8)
+        r_four = tiles("r_four", 2, [P, 2, QW, 4], BF16)
+        r_codes = tiles("r_codes", 2 * NQ, [P, 2 * QW], U32)
+        r_planes = tiles("r_planes", 2 * NQ, [P, 2 * QW], U8)
+        full = tiles("full", 4, [P, 2, 2, P, 2], BF16)
+        f_four = tiles("f_four", 2, [P, GL, P, 4], BF16)
+        f_codes = tiles("f_codes", NT, [P, GL * P], U32)
+        f_planes = tiles("f_planes", NT, [P, GL * P], U8)
+        left = tiles("left", NQ * NPAIR, [P, 2, QW], F32)
+        gained = tiles("gained", 3, [P, 2, QW], F32)
+        acc = [psum.tile([P, 512], F32, name="acc%d" % k) for k in range(4)]
+        turn_bank = [psum.tile([P, 2, 2, P], F32, name="turn%d" % k) for k in range(4)]
 
         c_v = C_bytes.rearrange("(p i) k -> p i k", i=NT)
         s_v = slopes.rearrange("(p i) l -> p i l", i=NT)
         p_v = prev.rearrange("(p i) a -> p i a", i=NT)
         o_v = out.rearrange("(p i) a -> p i a", i=NT)
         r_v = R_bytes.rearrange("(i p) l -> p i l", p=P)
+        g_v = G_words.rearrange("g p n -> p g n")
 
-        make_identity(nc, ident[:])
+        def load_c(m):
+            count = min(3, NT - 3 * m)
+            nc.sync.dma_start(out=c_raw[m][:, :count, :], in_=c_v[:, 3 * m : 3 * m + count, :])
+
+        def load_g(n):
+            nc.sync.dma_start(out=g_words[n][:].bitcast(I32), in_=g_v[:, :, 1024 * n : 1024 * (n + 1)].bitcast(I32))
+
+        def load_s(i):
+            nc.sync.dma_start(out=s_sb[i][:], in_=s_v[:, i, :])
+
+        def load_r(h):
+            q, half = h // 2, h % 2
+            nc.sync.dma_start(out=r_raw[h][:], in_=r_v[:, 2 * q : 2 * q + 2, SPAN * half : SPAN * (half + 1)])
+
+        def load_prev(half, part):
+            rows = slice(4 * part, 4 * part + 4)
+            nc.sync.dma_start(out=prev_sb[2 * half + part][:], in_=p_v[:, rows, 512 * half : 512 * (half + 1)])
+
         nc.vector.memset(g_sc[:].rearrange("p g n -> p (g n)").bitcast(I32), 0)
-
-        nc.scalar.dma_start(out=r_sc[:], in_=R_scale.rearrange("i j -> (i j)").partition_broadcast(P))
+        make_identity(nc, ident[:])
+        load_c(0)
+        nc.sync.dma_start(out=c_sc[:], in_=C_scale.rearrange("(p i) j -> p i j", i=NT))
+        nc.sync.dma_start(out=r_sc[:], in_=R_scale.rearrange("i j -> (i j)").partition_broadcast(P))
+        load_r(0)
         for q in range(4):
             nc.scalar.dma_start(
                 out=g_sc[32 * q : 32 * q + 4, :, :].bitcast(I32),
                 in_=G_scales[:, 4 * q : 4 * q + 4, :].rearrange("g q n -> q g n").bitcast(I32),
             )
-        nc.sync.dma_start(out=c_sc[:], in_=C_scale.rearrange("(p i) j -> p i j", i=NT))
-        nc.sync.dma_start(out=c_raw[:, 0:2, :], in_=c_v[:, 0:2, :])
-        nc.sync.dma_start(out=g_words[:, :, 0:1024].bitcast(I32), in_=G_words.rearrange("g p n -> p g n")[:, :, 0:1024].bitcast(I32))
-        nc.sync.dma_start(out=s_sb[:, 0, :], in_=s_v[:, 0, :])
-        nc.sync.dma_start(out=g_words[:, :, 1024:2048].bitcast(I32), in_=G_words.rearrange("g p n -> p g n")[:, :, 1024:2048].bitcast(I32))
-        nc.sync.dma_start(out=g_words[:, :, 2048:3072].bitcast(I32), in_=G_words.rearrange("g p n -> p g n")[:, :, 2048:3072].bitcast(I32))
-        nc.sync.dma_start(out=g_words[:, :, 3072:4096].bitcast(I32), in_=G_words.rearrange("g p n -> p g n")[:, :, 3072:4096].bitcast(I32))
-        nc.sync.dma_start(out=r_raw[:, 0:1, :], in_=r_v[:, 0:1, :])
-        nc.sync.dma_start(out=s_sb[:, 1, :], in_=s_v[:, 1, :])
-        nc.sync.dma_start(out=r_raw[:, 1:2, :], in_=r_v[:, 1:2, :])
-        nc.sync.dma_start(out=c_raw[:, 2:5, :], in_=c_v[:, 2:5, :])
-        nc.sync.dma_start(out=r_raw[:, 2:3, :], in_=r_v[:, 2:3, :])
-        nc.sync.dma_start(out=s_sb[:, 2, :], in_=s_v[:, 2, :])
+        load_g(0)
+        load_g(1)
+        load_s(0)
+        load_g(2)
+        load_g(3)
+        load_c(1)
+        load_s(1)
+        load_r(1)
         nc.sync.dma_start(out=leak_sb[:], in_=leak.partition_broadcast(P))
-        nc.sync.dma_start(out=prev_sb[:, 0:2, :], in_=p_v[:, 0:2, :])
-        nc.sync.dma_start(out=r_raw[:, 3:4, :], in_=r_v[:, 3:4, :])
-        nc.sync.dma_start(out=s_sb[:, 3, :], in_=s_v[:, 3, :])
-        nc.sync.dma_start(out=r_raw[:, 4:6, :], in_=r_v[:, 4:6, :])
-        nc.sync.dma_start(out=prev_sb[:, 2:4, :], in_=p_v[:, 2:4, :])
-        nc.sync.dma_start(out=c_raw[:, 5:8, :], in_=c_v[:, 5:8, :])
-        nc.sync.dma_start(out=s_sb[:, 4, :], in_=s_v[:, 4, :])
-        nc.sync.dma_start(out=r_raw[:, 6:8, :], in_=r_v[:, 6:8, :])
-        nc.sync.dma_start(out=s_sb[:, 5, :], in_=s_v[:, 5, :])
+        load_prev(0, 0)
+        load_s(2)
+        load_prev(0, 1)
+        load_c(2)
+        load_s(3)
+        load_r(2)
+        load_prev(1, 0)
+        load_s(4)
+        load_prev(1, 1)
+        load_s(5)
+        load_r(3)
+        load_s(6)
+        load_r(4)
+        load_s(7)
         nc.sync.dma_start(out=gain_sb[:], in_=gain.partition_broadcast(P))
-        nc.sync.dma_start(out=prev_sb[:, 4:8, :], in_=p_v[:, 4:8, :])
-        nc.sync.dma_start(out=s_sb[:, 6, :], in_=s_v[:, 6, :])
-        nc.sync.dma_start(out=s_sb[:, 7, :], in_=s_v[:, 7, :])
-        def widen(dst, raw, scale, on_vector):
-            if on_vector:
-                nc.vector.tensor_scalar(out=dst, in0=raw.bitcast(FP8), scalar1=scale, scalar2=None, op0=MULT)
-            else:
-                nc.scalar.activation(out=dst, in_=raw.bitcast(FP8), func=COPY, scale=scale)
+        load_r(5)
+        load_r(6)
+        load_r(7)
 
-        def turn(values, groups, dst):
-            words = values.bitcast(F32)
-            for g0 in range(0, groups, 2):
-                bank = psum.tile([P, 2, 2, P], F32, tag="turn", bufs=3, name="bank")
-                for g in range(2):
-                    for u in range(2):
-                        w0 = 256 * (g0 + g) + u
-                        nc.tensor.transpose(bank[:, g, u, :], words[:, w0 : w0 + 255 : 2], ident[:])
-                nc.scalar.copy(
-                    out=dst[:, g0 : g0 + 2, :, :].bitcast(F32),
-                    in_=bank[:].rearrange("p g u r -> p g r u"),
-                )
+        order = {}
 
-        c_four = {}
-        c_wide = {}
+        def strip_source(strip):
+            kind, k = strip
+            if kind == "c":
+                return c_raw[k // 3][:, k % 3, :], c_sc[:, k, :]
+            q, half, row = k // 4, (k // 2) % 2, k % 2
+            first = (2 * q + row) * (L // P) + half * (SPAN // P)
+            return r_raw[k // 2][:, row, :], r_sc[:, first : first + SPAN // P]
 
-        def widen_c(i, on_vector):
-            c_wide[i] = work.tile([P, A], BF16, tag="c_wide", bufs=2, align_bytes=64, name="c_w")
-            for j in range(A // P):
+        def widen(strip, on_vector):
+            order[strip] = len(order)
+            raw, scale = strip_source(strip)
+            dst = wide[order[strip] % len(wide)]
+            for j in range(SPAN // P):
                 k = slice(P * j, P * (j + 1))
-                widen(c_wide[i][:, k], c_raw[:, i, k], c_sc[:, i, j : j + 1], on_vector)
+                if on_vector:
+                    nc.vector.tensor_scalar(
+                        out=dst[:, k], in0=raw[:, k].bitcast(FP8), scalar1=scale[:, j : j + 1], scalar2=None, op0=MULT
+                    )
+                else:
+                    nc.scalar.activation(out=dst[:, k], in_=raw[:, k].bitcast(FP8), func=COPY, scale=scale[:, j : j + 1])
 
-        def turn_c(i):
-            c_four[i] = work.tile([P, GA, P, 4], BF16, tag="c_four", bufs=2, align_bytes=64, name="c_f")
-            turn(c_wide[i][:], GA, c_four[i])
+        turned = []
+
+        def next_bank():
+            turned.append(len(turned))
+            return turn_bank[turned[-1] % len(turn_bank)]
+
+        def empty(bank, dst):
+            nc.scalar.copy(out=dst.bitcast(F32), in_=bank[:].rearrange("p g u r -> p g r u"))
+
+        def turn_strip(strip):
+            kind, k = strip
+            words = wide[order[strip] % len(wide)][:].bitcast(F32)
+            bank = next_bank()
+            for g in range(2):
+                for u in range(2):
+                    w0 = 256 * g + u
+                    nc.tensor.transpose(bank[:, g, u, :], words[:, w0 : w0 + 255 : 2], ident[:])
+            if kind == "c":
+                empty(bank, c_four[k % 2][:])
+            else:
+                row = k % 2
+                empty(bank, r_four[(k // 2) % 2][:, :, P * row : P * (row + 1), :])
+
+        def quantize(codes, planes, four):
+            nc.vector.quantize_mx(out=codes[:].bitcast(FP8X4), scales=planes[:], in_=four[:].rearrange("p g r j -> p (g r j)"))
 
         def quant_c(i):
-            nc.vector.quantize_mx(
-                out=c_codes[:, i, :].bitcast(FP8X4),
-                scales=c_planes[:, i, :],
-                in_=c_four[i][:].rearrange("p g r j -> p (g r j)"),
-            )
+            quantize(c_codes[i % 3], c_planes[i % 3], c_four[i % 2])
 
-        r_four = {}
-        r_wide = {}
+        def quant_r(h):
+            quantize(r_codes[h], r_planes[h], r_four[h % 2])
 
-        def widen_r(i, on_vector):
-            r_wide[i] = work.tile([P, L], BF16, tag="r_wide", bufs=3, align_bytes=64, name="r_w")
-            for j in range(L // P):
-                k = slice(P * j, P * (j + 1))
-                s = i * (L // P) + j
-                widen(r_wide[i][:, k], r_raw[:, i, k], r_sc[:, s : s + 1], on_vector)
-
-        def turn_r(i):
-            r_four[i] = work.tile([P, GL, P, 4], BF16, tag="r_four", bufs=3, align_bytes=64, name="r_f")
-            turn(r_wide[i][:], GL, r_four[i])
-
-        def quant_r(i):
-            cols = slice(P * i, P * (i + 1))
-            for g in range(GL):
-                nc.vector.quantize_mx(
-                    out=r_codes[:, g, cols].bitcast(FP8X4),
-                    scales=r_planes[:, g, cols],
-                    in_=r_four[i][:, g, :, :].rearrange("p r j -> p (r j)"),
-                )
-
-        full = {}
-        f_four = {}
+        def quant_f(i):
+            quantize(f_codes[i], f_planes[i], f_four[i % 2])
 
         def mirror(i):
-            full[i] = work.tile([P, GL, 2, P, 2], BF16, tag="full", bufs=2, align_bytes=64, name="full_t")
             for n in range(NL):
-                acc = psum.tile([P, 512], F32, tag="acc", bufs=3, name="acc")
                 for g in range(GA):
                     nc.tensor.matmul_mx(
-                        out=acc[:],
-                        lhsT=c_codes[:, i, P * g : P * (g + 1)].bitcast(FP8X4),
-                        lhsT_scale=c_planes[:, i, P * g : P * (g + 1)],
-                        rhs=g_words[:, g, 1024 * n : 1024 * (n + 1)].bitcast(FP4X4),
+                        out=acc[n][:],
+                        lhsT=c_codes[i % 3][:, P * g : P * (g + 1)].bitcast(FP8X4),
+                        lhsT_scale=c_planes[i % 3][:, P * g : P * (g + 1)],
+                        rhs=g_words[n][:, g, :].bitcast(FP4X4),
                         rhs_scale=g_sc[:, g, 512 * n : 512 * (n + 1)],
                         start=(g == 0),
                         stop=(g == GA - 1),
                     )
                 nc.vector.tensor_tensor(
-                    out=full[i][:, n, :, :, :],
-                    in0=acc[:].rearrange("p (w u e) -> p u w e", u=2, e=2),
-                    in1=s_sb[:, i, 512 * n : 512 * (n + 1)].rearrange("p (w u e) -> p u w e", u=2, e=2),
+                    out=full[(2 * i + n // 2) % 4][:, n % 2, :, :, :],
+                    in0=acc[n][:].rearrange("p (w u e) -> p u w e", u=2, e=2),
+                    in1=s_sb[i][:, 512 * n : 512 * (n + 1)].rearrange("p (w u e) -> p u w e", u=2, e=2),
                     op=ADD,
                 )
 
         def turn_f(i):
-            f_four[i] = work.tile([P, GL, P, 4], BF16, tag="f_four", bufs=2, align_bytes=64, name="f_f")
-            words = full[i][:].rearrange("p g u w e -> p (g u w e)").bitcast(F32)
-            for g0 in range(0, GL, 2):
-                bank = psum.tile([P, 2, 2, P], F32, tag="turn", bufs=3, name="bank")
+            for h in range(2):
+                words = full[(2 * i + h) % 4][:].rearrange("p g u w e -> p (g u w e)").bitcast(F32)
+                bank = next_bank()
                 for g in range(2):
                     for u in range(2):
-                        w0 = P * (2 * (g0 + g) + u)
+                        w0 = P * (2 * g + u)
                         nc.tensor.transpose(bank[:, g, u, :], words[:, w0 : w0 + P], ident[:])
-                nc.scalar.copy(
-                    out=f_four[i][:, g0 : g0 + 2, :, :].bitcast(F32),
-                    in_=bank[:].rearrange("p g u r -> p g r u"),
-                )
+                empty(bank, f_four[i % 2][:, 2 * h : 2 * h + 2, :, :])
 
-        def quant_f(i):
-            nc.vector.quantize_mx(
-                out=f_codes[:, i, :].bitcast(FP8X4),
-                scales=f_planes[:, i, :],
-                in_=f_four[i][:].rearrange("p g r j -> p (g r j)"),
+        def along(row, q):
+            return row[:, QW * q : QW * (q + 1)].unsqueeze(1).to_broadcast([P, 2, QW])
+
+        def leaky(unit):
+            q, m = unit // NPAIR, unit % NPAIR
+            src = prev_sb[2 * (q // 2) + m // 2][:, 2 * (m % 2) : 2 * (m % 2) + 2, QW * (q % 2) : QW * (q % 2 + 1)]
+            nc.vector.tensor_tensor(out=left[unit][:], in0=src, in1=along(leak_sb, q), op=MULT)
+
+        def react(unit):
+            q, m = unit // NPAIR, unit % NPAIR
+            bank = acc[unit % 4]
+            for side in range(2):
+                i = 2 * m + side
+                for g in range(GL):
+                    cols = slice(QW * (g % 2), QW * (g % 2 + 1))
+                    nc.tensor.matmul_mx(
+                        out=bank[:, QW * side : QW * (side + 1)],
+                        lhsT=f_codes[i][:, P * g : P * (g + 1)].bitcast(FP8X4),
+                        lhsT_scale=f_planes[i][:, P * g : P * (g + 1)],
+                        rhs=r_codes[2 * q + g // 2][:, cols].bitcast(FP8X4),
+                        rhs_scale=r_planes[2 * q + g // 2][:, cols],
+                        start=(g == 0),
+                        stop=(g == GL - 1),
+                    )
+            nc.vector.tensor_tensor(
+                out=gained[unit % 3][:], in0=bank[:].rearrange("p (s a) -> p s a", s=2), in1=along(gain_sb, q), op=MULT
             )
 
-        left = {}
+        def finish(unit):
+            q, m = unit // NPAIR, unit % NPAIR
+            nc.vector.tensor_tensor(out=left[unit][:], in0=gained[unit % 3][:], in1=left[unit][:], op=ADD)
+            nc.sync.dma_start(out=o_v[:, 2 * m : 2 * m + 2, QW * q : QW * (q + 1)], in_=left[unit][:])
 
-        def leaky(i):
-            left[i] = work.tile([P, A], F32, tag="left", bufs=8, align_bytes=64, name="left_t")
-            nc.vector.tensor_tensor(out=left[i][:], in0=prev_sb[:, i, :], in1=leak_sb[:], op=MULT)
+        runs = []
+        taken = HEAD_R
+        for s in range(NT):
+            run = []
+            if s + HEAD_C < NT:
+                run.append(("c", s + HEAD_C))
+            if (s % 2 == 0 and s > 0) or s + HEAD_C >= NT - 1:
+                run.append(("r", taken))
+                taken = taken + 1
+            runs.append(run)
+        while taken < NRU:
+            runs.append([("r", k) for k in range(taken, min(taken + 2, NRU))])
+            taken = taken + 2
 
-        def react(i, c):
-            cols = slice(512 * c, 512 * (c + 1))
-            acc2 = psum.tile([P, 512], F32, tag="acc2", bufs=2, name="acc2")
-            for g in range(GL):
-                nc.tensor.matmul_mx(
-                    out=acc2[:],
-                    lhsT=f_codes[:, i, P * g : P * (g + 1)].bitcast(FP8X4),
-                    lhsT_scale=f_planes[:, i, P * g : P * (g + 1)],
-                    rhs=r_codes[:, g, cols].bitcast(FP8X4),
-                    rhs_scale=r_planes[:, g, cols],
-                    start=(g == 0),
-                    stop=(g == GL - 1),
-                )
-            gained[i, c] = work.tile([P, 512], F32, tag="gained", bufs=4, align_bytes=64, name="gained_t")
-            nc.vector.tensor_tensor(out=gained[i, c][:], in0=acc2[:], in1=gain_sb[:, cols], op=MULT)
+        def run_of(s):
+            return runs[s] if s < len(runs) else []
 
-        gained = {}
+        def ready_halves(s):
+            return (HEAD_R + sum(1 for r in runs[:s] for kind, k in r if kind == "r")) // 2
 
-        def finish(i, c):
-            cols = slice(512 * c, 512 * (c + 1))
-            nc.vector.tensor_tensor(out=left[i][:, cols], in0=gained[i, c][:], in1=left[i][:, cols], op=ADD)
-            nc.sync.dma_start(out=o_v[:, i, cols], in_=left[i][:, cols])
+        widen(("c", 0), True)
+        widen(("c", 2), False)
+        turn_strip(("c", 0))
+        widen(("c", 1), True)
+        turn_strip(("c", 1))
+        for k in range(HEAD_R):
+            widen(("r", k), True)
+        quant_c(0)
+        for k in range(HEAD_R):
+            turn_strip(("r", k))
+        quant_c(1)
+        for strip in run_of(1):
+            widen(strip, False)
 
+        units = NQ * NPAIR
+        quantized = []
+        left_done = []
 
-        V_R = (0, 1)
-        TURN_R = [[0], [1, 2], [3], [4], [5], [6], [7], []]
-        REACT = [[], [], [], [], [(0, 0),(1, 0),(2, 0)], [(3, 0),(4, 0)], [(5, 0)], [(6, 0)], [(0, 1),(1, 1),(2, 1),(3, 1),(4, 1),(5, 1),(6, 1), (7, 0), (7, 1)]]
-        LEAKY = [[], [0], [1], [2], [3, 4], [5], [6], [7]]
-        if True:
-            widen_c(0, True)
-            widen_c(1, False)
-            turn_c(0)
-            quant_c(0)
-            turn_c(1)
-            quant_c(1)
-            widen_c(2, False)
-            pend_q = []
-            pend_f = []
-            for i in TURN_R[0]:
-                widen_r(i, i in V_R)
-            for s in range(NT):
-                mirror(s)
-                for i, c in REACT[s]:
-                    react(i, c)
-                if s + 2 < NT:
-                    turn_c(s + 2)
-                for i in TURN_R[s]:
-                    turn_r(i)
-                turn_f(s)
-                if s + 3 < NT:
-                    widen_c(s + 3, False)
-                if s + 1 < NT:
-                    for i in TURN_R[s + 1]:
-                        widen_r(i, i in V_R)
-                for i, c in REACT[s]:
-                    finish(i, c)
-                if s + 2 < NT:
-                    quant_c(s + 2)
-                for i in LEAKY[s]:
-                    leaky(i)
-                for i in TURN_R[s]:
-                    quant_r(i)
-                quant_f(s)
-            last = None
-            for i, c in REACT[NT]:
-                react(i, c)
-                if last:
-                    finish(*last)
-                last = (i, c)
-            finish(*last)
+        def catch_up_r(s):
+            while len(quantized) < ready_halves(s):
+                quant_r(len(quantized))
+                quantized.append(s)
+
+        def more_left(count):
+            for k in range(count):
+                if len(left_done) < units:
+                    leaky(len(left_done))
+                    left_done.append(k)
+
+        for s in range(NT):
+            mirror(s)
+            if s >= 2:
+                quant_f(s - 2)
+            catch_up_r(s)
+            if s >= 1:
+                more_left(2)
+            for strip in run_of(s):
+                turn_strip(strip)
+            if s >= 1:
+                turn_f(s - 1)
+            if s + HEAD_C < NT:
+                quant_c(s + HEAD_C)
+            for strip in run_of(s + 2):
+                widen(strip, False)
+
+        for unit in range(units):
+            s = NT + unit // 2
+            react(unit)
+            if unit >= 1:
+                finish(unit - 1)
+            if unit % 2 == 0:
+                if unit == 0:
+                    quant_f(NT - 2)
+                catch_up_r(s)
+                if unit == 0:
+                    turn_f(NT - 1)
+                for strip in run_of(s):
+                    turn_strip(strip)
+                for strip in run_of(s + 2):
+                    widen(strip, False)
+            else:
+                catch_up_r(s + 1)
+                if unit == 1:
+                    quant_f(NT - 1)
+                more_left(1)
+        finish(units - 1)

@@ -29,6 +29,8 @@ NQ = A // QW
 NPAIR = NT // 2
 NRU = (A // P) * (L // SPAN)
 HEAD_C = 2
+FIRST_SHARED = 3
+POOL_COLS = 384
 HEAD_R = 2
 
 
@@ -56,7 +58,6 @@ def tile_leaky_slope_reconstructor_d6_kernel(
         leak_sb = tiles("leak_sb", 1, [P, A], BF16)[0]
         ident = tiles("ident", 1, [P, P], F32)[0]
         wide = tiles("wide", 8, [P, SPAN], BF16)
-        c_four = tiles("c_four", 2, [P, GA, P, 4], BF16)
         c_codes = tiles("c_codes", 3, [P, GA * P], U32)
         c_planes = tiles("c_planes", 3, [P, GA * P], U8)
         r_four = tiles("r_four", 2, [P, 2, QW, 4], BF16)
@@ -66,7 +67,8 @@ def tile_leaky_slope_reconstructor_d6_kernel(
         f_four = tiles("f_four", 2, [P, GL, P, 4], BF16)
         f_codes = tiles("f_codes", NT, [P, GL * P], U32)
         f_planes = tiles("f_planes", NT, [P, GL * P], U8)
-        left = tiles("left", NQ * NPAIR, [P, 2, QW], F32)
+        left = tiles("left", 2 * NPAIR, [P, 2, 2 * QW], F32)
+        c_head = tiles("c_head", FIRST_SHARED, [P, 2 * QW], F32)
         gained = tiles("gained", 3, [P, 2, QW], F32)
         acc = [psum.tile([P, 512], F32, name="acc%d" % k) for k in range(4)]
         turn_bank = [psum.tile([P, 2, 2, P], F32, name="turn%d" % k) for k in range(4)]
@@ -158,6 +160,10 @@ def tile_leaky_slope_reconstructor_d6_kernel(
                 else:
                     nc.scalar.activation(out=dst[:, k], in_=raw[:, k].bitcast(FP8), func=COPY, scale=scale[:, j : j + 1])
 
+        def c_four(i):
+            room = c_head[i][:] if i < FIRST_SHARED else left[i - FIRST_SHARED][:, 0, :]
+            return room.bitcast(BF16).rearrange("p (g r j) -> p g r j", g=GA, j=4)
+
         turned = []
 
         def next_bank():
@@ -176,22 +182,22 @@ def tile_leaky_slope_reconstructor_d6_kernel(
                     w0 = 256 * g + u
                     nc.tensor.transpose(bank[:, g, u, :], words[:, w0 : w0 + 255 : 2], ident[:])
             if kind == "c":
-                empty(bank, c_four[k % 2][:])
+                empty(bank, c_four(k))
             else:
                 row = k % 2
                 empty(bank, r_four[(k // 2) % 2][:, :, P * row : P * (row + 1), :])
 
         def quantize(codes, planes, four):
-            nc.vector.quantize_mx(out=codes[:].bitcast(FP8X4), scales=planes[:], in_=four[:].rearrange("p g r j -> p (g r j)"))
+            nc.vector.quantize_mx(out=codes[:].bitcast(FP8X4), scales=planes[:], in_=four.rearrange("p g r j -> p (g r j)"))
 
         def quant_c(i):
-            quantize(c_codes[i % 3], c_planes[i % 3], c_four[i % 2])
+            quantize(c_codes[i % 3], c_planes[i % 3], c_four(i))
 
         def quant_r(h):
-            quantize(r_codes[h], r_planes[h], r_four[h % 2])
+            quantize(r_codes[h], r_planes[h], r_four[h % 2][:])
 
         def quant_f(i):
-            quantize(f_codes[i], f_planes[i], f_four[i % 2])
+            quantize(f_codes[i], f_planes[i], f_four[i % 2][:])
 
         def mirror(i):
             for n in range(NL):
@@ -225,10 +231,15 @@ def tile_leaky_slope_reconstructor_d6_kernel(
         def along(row, q):
             return row[:, QW * q : QW * (q + 1)].unsqueeze(1).to_broadcast([P, 2, QW])
 
-        def leaky(unit):
+        def leaky(k, engine, first, end):
+            half, m = k // NPAIR, k % NPAIR
+            src = prev_sb[2 * half + m // 2][:, 2 * (m % 2) : 2 * (m % 2) + 2, first:end]
+            rates = leak_sb[:, 2 * QW * half + first : 2 * QW * half + end].unsqueeze(1).to_broadcast([P, 2, end - first])
+            engine.tensor_tensor(out=left[k][:, :, first:end], in0=src, in1=rates, op=MULT)
+
+        def left_of(unit):
             q, m = unit // NPAIR, unit % NPAIR
-            src = prev_sb[2 * (q // 2) + m // 2][:, 2 * (m % 2) : 2 * (m % 2) + 2, QW * (q % 2) : QW * (q % 2 + 1)]
-            nc.vector.tensor_tensor(out=left[unit][:], in0=src, in1=along(leak_sb, q), op=MULT)
+            return left[NPAIR * (q // 2) + m][:, :, QW * (q % 2) : QW * (q % 2 + 1)]
 
         def react(unit):
             q, m = unit // NPAIR, unit % NPAIR
@@ -252,8 +263,8 @@ def tile_leaky_slope_reconstructor_d6_kernel(
 
         def finish(unit):
             q, m = unit // NPAIR, unit % NPAIR
-            nc.vector.tensor_tensor(out=left[unit][:], in0=gained[unit % 3][:], in1=left[unit][:], op=ADD)
-            nc.sync.dma_start(out=o_v[:, 2 * m : 2 * m + 2, QW * q : QW * (q + 1)], in_=left[unit][:])
+            nc.vector.tensor_tensor(out=left_of(unit), in0=gained[unit % 3][:], in1=left_of(unit), op=ADD)
+            nc.sync.dma_start(out=o_v[:, 2 * m : 2 * m + 2, QW * q : QW * (q + 1)], in_=left_of(unit))
 
         runs = []
         taken = HEAD_R
@@ -291,32 +302,30 @@ def tile_leaky_slope_reconstructor_d6_kernel(
 
         units = NQ * NPAIR
         quantized = []
-        left_done = []
 
         def catch_up_r(s):
             while len(quantized) < ready_halves(s):
                 quant_r(len(quantized))
                 quantized.append(s)
 
-        def more_left(count):
-            for k in range(count):
-                if len(left_done) < units:
-                    leaky(len(left_done))
-                    left_done.append(k)
-
         for s in range(NT):
+            shared = s + HEAD_C - FIRST_SHARED
             mirror(s)
+            if 1 <= shared <= NT - FIRST_SHARED:
+                leaky(shared - 1, nc.vector, POOL_COLS, 2 * QW)
             if s >= 2:
                 quant_f(s - 2)
             catch_up_r(s)
-            if s >= 1:
-                more_left(2)
             for strip in run_of(s):
                 turn_strip(strip)
             if s >= 1:
                 turn_f(s - 1)
             if s + HEAD_C < NT:
                 quant_c(s + HEAD_C)
+                if shared >= 0:
+                    leaky(shared, nc.gpsimd, 0, POOL_COLS)
+            else:
+                leaky(shared, nc.vector, 0, 2 * QW)
             for strip in run_of(s + 2):
                 widen(strip, False)
 
@@ -339,5 +348,6 @@ def tile_leaky_slope_reconstructor_d6_kernel(
                 catch_up_r(s + 1)
                 if unit == 1:
                     quant_f(NT - 1)
-                more_left(1)
+                if unit == 3:
+                    leaky(2 * NPAIR - 1, nc.vector, 0, 2 * QW)
         finish(units - 1)

@@ -28,10 +28,12 @@ QW = 256
 NQ = A // QW
 NPAIR = NT // 2
 NRU = (A // P) * (L // SPAN)
-HEAD_C = 2
+HEAD_C = 3
+C_LOADS = ((0, 1), (1, 5), (5, 8))
+NGAINED = 6
+PAIRED_END = 11
+SHARED_F = NT - 4
 FIRST_SHARED = 3
-POOL_COLS = 384
-HEAD_R = 2
 
 
 def tile_leaky_slope_reconstructor_d6_kernel(
@@ -46,14 +48,14 @@ def tile_leaky_slope_reconstructor_d6_kernel(
         def tiles(name, count, shape, dtype):
             return [keep.tile(shape, dtype, align_bytes=64, name="%s%d" % (name, k)) for k in range(count)]
 
-        c_raw = tiles("c_raw", 3, [P, 3, A], U8)
+        c_raw = [tiles("c_raw%d_" % first, 1, [P, end - first, A], U8)[0] for first, end in C_LOADS]
         c_sc = tiles("c_sc", 1, [P, NT, A // P], F32)[0]
-        g_words = tiles("g_words", NL, [P, GA, 1024], U8)
+        g_words = tiles("g_words", NL // 2, [P, GA, L], U8)
         g_sc = tiles("g_sc", 1, [P, GA, L], U8)[0]
         r_raw = tiles("r_raw", 2 * NQ, [P, 2, SPAN], U8)
         r_sc = tiles("r_sc", 1, [P, (A // P) * (L // P)], F32)[0]
         s_sb = tiles("s_sb", NT, [P, L], BF16)
-        prev_sb = tiles("prev_sb", 4, [P, NT // 2, A // 2], BF16)
+        prev_sb = tiles("prev_sb", 2 * NPAIR, [P, 2, 2 * QW], BF16)
         gain_sb = tiles("gain_sb", 1, [P, A], BF16)[0]
         leak_sb = tiles("leak_sb", 1, [P, A], BF16)[0]
         ident = tiles("ident", 1, [P, P], F32)[0]
@@ -64,12 +66,12 @@ def tile_leaky_slope_reconstructor_d6_kernel(
         r_codes = tiles("r_codes", 2 * NQ, [P, 2 * QW], U32)
         r_planes = tiles("r_planes", 2 * NQ, [P, 2 * QW], U8)
         full = tiles("full", 4, [P, 2, 2, P, 2], BF16)
-        f_four = tiles("f_four", 2, [P, GL, P, 4], BF16)
+        f_ring = tiles("f_ring", 2, [P, 2, 2 * QW], F32)
         f_codes = tiles("f_codes", NT, [P, GL * P], U32)
         f_planes = tiles("f_planes", NT, [P, GL * P], U8)
         left = tiles("left", 2 * NPAIR, [P, 2, 2 * QW], F32)
         c_head = tiles("c_head", FIRST_SHARED, [P, 2 * QW], F32)
-        gained = tiles("gained", 3, [P, 2, QW], F32)
+        gained = tiles("gained", NGAINED, [P, 2, QW], F32)
         acc = [psum.tile([P, 512], F32, name="acc%d" % k) for k in range(4)]
         turn_bank = [psum.tile([P, 2, 2, P], F32, name="turn%d" % k) for k in range(4)]
 
@@ -81,11 +83,11 @@ def tile_leaky_slope_reconstructor_d6_kernel(
         g_v = G_words.rearrange("g p n -> p g n")
 
         def load_c(m):
-            count = min(3, NT - 3 * m)
-            nc.sync.dma_start(out=c_raw[m][:, :count, :], in_=c_v[:, 3 * m : 3 * m + count, :])
+            first, end = C_LOADS[m]
+            nc.sync.dma_start(out=c_raw[m][:], in_=c_v[:, first:end, :])
 
         def load_g(n):
-            nc.sync.dma_start(out=g_words[n][:].bitcast(I32), in_=g_v[:, :, 1024 * n : 1024 * (n + 1)].bitcast(I32))
+            nc.sync.dma_start(out=g_words[n][:].bitcast(I32), in_=g_v[:, :, L * n : L * (n + 1)].bitcast(I32))
 
         def load_s(i):
             nc.sync.dma_start(out=s_sb[i][:], in_=s_v[:, i, :])
@@ -94,55 +96,44 @@ def tile_leaky_slope_reconstructor_d6_kernel(
             q, half = h // 2, h % 2
             nc.sync.dma_start(out=r_raw[h][:], in_=r_v[:, 2 * q : 2 * q + 2, SPAN * half : SPAN * (half + 1)])
 
-        def load_prev(half, part):
-            rows = slice(4 * part, 4 * part + 4)
-            nc.sync.dma_start(out=prev_sb[2 * half + part][:], in_=p_v[:, rows, 512 * half : 512 * (half + 1)])
+        def load_prev(k):
+            half, m = k // NPAIR, k % NPAIR
+            nc.sync.dma_start(out=prev_sb[k][:], in_=p_v[:, 2 * m : 2 * m + 2, 2 * QW * half : 2 * QW * (half + 1)])
 
         nc.vector.memset(g_sc[:].rearrange("p g n -> p (g n)").bitcast(I32), 0)
         make_identity(nc, ident[:])
-        load_c(0)
         nc.sync.dma_start(out=c_sc[:], in_=C_scale.rearrange("(p i) j -> p i j", i=NT))
-        nc.sync.dma_start(out=r_sc[:], in_=R_scale.rearrange("i j -> (i j)").partition_broadcast(P))
-        load_r(0)
+        load_c(0)
+        load_c(1)
+        load_g(0)
         for q in range(4):
             nc.scalar.dma_start(
                 out=g_sc[32 * q : 32 * q + 4, :, :].bitcast(I32),
                 in_=G_scales[:, 4 * q : 4 * q + 4, :].rearrange("g q n -> q g n").bitcast(I32),
             )
-        load_g(0)
         load_g(1)
         load_s(0)
-        load_g(2)
-        load_g(3)
-        load_c(1)
+        nc.sync.dma_start(out=r_sc[:], in_=R_scale.rearrange("i j -> (i j)").partition_broadcast(P))
+        load_r(0)
         load_s(1)
-        load_r(1)
-        nc.sync.dma_start(out=leak_sb[:], in_=leak.partition_broadcast(P))
-        load_prev(0, 0)
-        load_s(2)
-        load_prev(0, 1)
         load_c(2)
-        load_s(3)
-        load_r(2)
-        load_prev(1, 0)
-        load_s(4)
-        load_prev(1, 1)
-        load_s(5)
-        load_r(3)
-        load_s(6)
-        load_r(4)
-        load_s(7)
+        nc.sync.dma_start(out=leak_sb[:], in_=leak.partition_broadcast(P))
+        for s in range(2, NT):
+            load_prev(s - 2)
+            load_s(s)
+            if s in (2, 3):
+                load_prev(NT - 4 + s)
+            load_r(s - 1)
         nc.sync.dma_start(out=gain_sb[:], in_=gain.partition_broadcast(P))
-        load_r(5)
-        load_r(6)
-        load_r(7)
+        load_r(NT - 1)
 
         order = {}
 
         def strip_source(strip):
             kind, k = strip
             if kind == "c":
-                return c_raw[k // 3][:, k % 3, :], c_sc[:, k, :]
+                m = sum(1 for first, end in C_LOADS if end <= k)
+                return c_raw[m][:, k - C_LOADS[m][0], :], c_sc[:, k, :]
             q, half, row = k // 4, (k // 2) % 2, k % 2
             first = (2 * q + row) * (L // P) + half * (SPAN // P)
             return r_raw[k // 2][:, row, :], r_sc[:, first : first + SPAN // P]
@@ -163,6 +154,10 @@ def tile_leaky_slope_reconstructor_d6_kernel(
         def c_four(i):
             room = c_head[i][:] if i < FIRST_SHARED else left[i - FIRST_SHARED][:, 0, :]
             return room.bitcast(BF16).rearrange("p (g r j) -> p g r j", g=GA, j=4)
+
+        def f_four(i):
+            room = left[NT - FIRST_SHARED] if i == SHARED_F else f_ring[i % 2]
+            return room[:].rearrange("p s a -> p (s a)").bitcast(BF16).rearrange("p (g r j) -> p g r j", g=GL, j=4)
 
         turned = []
 
@@ -197,7 +192,7 @@ def tile_leaky_slope_reconstructor_d6_kernel(
             quantize(r_codes[h], r_planes[h], r_four[h % 2][:])
 
         def quant_f(i):
-            quantize(f_codes[i], f_planes[i], f_four[i % 2][:])
+            quantize(f_codes[i], f_planes[i], f_four(i))
 
         def mirror(i):
             for n in range(NL):
@@ -206,7 +201,7 @@ def tile_leaky_slope_reconstructor_d6_kernel(
                         out=acc[n][:],
                         lhsT=c_codes[i % 3][:, P * g : P * (g + 1)].bitcast(FP8X4),
                         lhsT_scale=c_planes[i % 3][:, P * g : P * (g + 1)],
-                        rhs=g_words[n][:, g, :].bitcast(FP4X4),
+                        rhs=g_words[n // 2][:, g, 1024 * (n % 2) : 1024 * (n % 2 + 1)].bitcast(FP4X4),
                         rhs_scale=g_sc[:, g, 512 * n : 512 * (n + 1)],
                         start=(g == 0),
                         stop=(g == GA - 1),
@@ -226,16 +221,15 @@ def tile_leaky_slope_reconstructor_d6_kernel(
                     for u in range(2):
                         w0 = P * (2 * g + u)
                         nc.tensor.transpose(bank[:, g, u, :], words[:, w0 : w0 + P], ident[:])
-                empty(bank, f_four[i % 2][:, 2 * h : 2 * h + 2, :, :])
+                empty(bank, f_four(i)[:, 2 * h : 2 * h + 2, :, :])
 
         def along(row, q):
             return row[:, QW * q : QW * (q + 1)].unsqueeze(1).to_broadcast([P, 2, QW])
 
         def leaky(k, engine, first, end):
-            half, m = k // NPAIR, k % NPAIR
-            src = prev_sb[2 * half + m // 2][:, 2 * (m % 2) : 2 * (m % 2) + 2, first:end]
-            rates = leak_sb[:, 2 * QW * half + first : 2 * QW * half + end].unsqueeze(1).to_broadcast([P, 2, end - first])
-            engine.tensor_tensor(out=left[k][:, :, first:end], in0=src, in1=rates, op=MULT)
+            base = 2 * QW * (k // NPAIR)
+            rates = leak_sb[:, base + first : base + end].unsqueeze(1).to_broadcast([P, 2, end - first])
+            engine.tensor_tensor(out=left[k][:, :, first:end], in0=prev_sb[k][:, :, first:end], in1=rates, op=MULT)
 
         def left_of(unit):
             q, m = unit // NPAIR, unit % NPAIR
@@ -258,21 +252,19 @@ def tile_leaky_slope_reconstructor_d6_kernel(
                         stop=(g == GL - 1),
                     )
             nc.vector.tensor_tensor(
-                out=gained[unit % 3][:], in0=bank[:].rearrange("p (s a) -> p s a", s=2), in1=along(gain_sb, q), op=MULT
+                out=gained[unit % NGAINED][:], in0=bank[:].rearrange("p (s a) -> p s a", s=2), in1=along(gain_sb, q), op=MULT
             )
 
-        def finish(unit):
+        def finish(unit, engine, result):
             q, m = unit // NPAIR, unit % NPAIR
-            nc.vector.tensor_tensor(out=left_of(unit), in0=gained[unit % 3][:], in1=left_of(unit), op=ADD)
-            nc.sync.dma_start(out=o_v[:, 2 * m : 2 * m + 2, QW * q : QW * (q + 1)], in_=left_of(unit))
+            engine.tensor_tensor(out=result, in0=gained[unit % NGAINED][:], in1=left_of(unit), op=ADD)
+            nc.sync.dma_start(out=o_v[:, 2 * m : 2 * m + 2, QW * q : QW * (q + 1)], in_=result)
 
         runs = []
-        taken = HEAD_R
+        taken = 0
         for s in range(NT):
-            run = []
-            if s + HEAD_C < NT:
-                run.append(("c", s + HEAD_C))
-            if (s % 2 == 0 and s > 0) or s + HEAD_C >= NT - 1:
+            run = [("c", s + HEAD_C)] if s + HEAD_C < NT else []
+            while len(run) < 1 + s % 2:
                 run.append(("r", taken))
                 taken = taken + 1
             runs.append(run)
@@ -284,21 +276,17 @@ def tile_leaky_slope_reconstructor_d6_kernel(
             return runs[s] if s < len(runs) else []
 
         def ready_halves(s):
-            return (HEAD_R + sum(1 for r in runs[:s] for kind, k in r if kind == "r")) // 2
+            return sum(1 for r in runs[:s] for kind, k in r if kind == "r") // 2
 
         widen(("c", 0), True)
-        widen(("c", 2), False)
         turn_strip(("c", 0))
         widen(("c", 1), True)
-        turn_strip(("c", 1))
-        for k in range(HEAD_R):
-            widen(("r", k), True)
+        widen(("c", 2), True)
         quant_c(0)
-        for k in range(HEAD_R):
-            turn_strip(("r", k))
+        widen(("c", 3), True)
+        turn_strip(("c", 1))
+        turn_strip(("c", 2))
         quant_c(1)
-        for strip in run_of(1):
-            widen(strip, False)
 
         units = NQ * NPAIR
         quantized = []
@@ -309,45 +297,49 @@ def tile_leaky_slope_reconstructor_d6_kernel(
                 quantized.append(s)
 
         for s in range(NT):
-            shared = s + HEAD_C - FIRST_SHARED
             mirror(s)
-            if 1 <= shared <= NT - FIRST_SHARED:
-                leaky(shared - 1, nc.vector, POOL_COLS, 2 * QW)
+            if s == 0:
+                for strip in run_of(1):
+                    widen(strip, False)
+            catch_up_r(s)
+            if 3 <= s <= 6:
+                leaky(NT - 2 + (s - 3) // 2, nc.vector, QW * ((s - 3) % 2), QW * ((s - 3) % 2 + 1))
             if s >= 2:
                 quant_f(s - 2)
-            catch_up_r(s)
+            if s - 2 == SHARED_F:
+                leaky(NT - FIRST_SHARED, nc.gpsimd, 0, 2 * QW)
+            if s + 2 < NT:
+                quant_c(s + 2)
+                if s + 2 >= FIRST_SHARED:
+                    leaky(s + 2 - FIRST_SHARED, nc.gpsimd, 0, 2 * QW)
             for strip in run_of(s):
                 turn_strip(strip)
             if s >= 1:
                 turn_f(s - 1)
-            if s + HEAD_C < NT:
-                quant_c(s + HEAD_C)
-                if shared >= 0:
-                    leaky(shared, nc.gpsimd, 0, POOL_COLS)
-            else:
-                leaky(shared, nc.vector, 0, 2 * QW)
             for strip in run_of(s + 2):
                 widen(strip, False)
 
-        for unit in range(units):
+        react(0)
+        catch_up_r(NT)
+        quant_f(NT - 2)
+        for unit in range(1, PAIRED_END, 2):
             s = NT + unit // 2
+            if unit == 1:
+                turn_f(NT - 1)
+            for strip in run_of(s):
+                turn_strip(strip)
+            for strip in run_of(s + 2):
+                widen(strip, False)
             react(unit)
-            if unit >= 1:
-                finish(unit - 1)
-            if unit % 2 == 0:
-                if unit == 0:
-                    quant_f(NT - 2)
-                catch_up_r(s)
-                if unit == 0:
-                    turn_f(NT - 1)
-                for strip in run_of(s):
-                    turn_strip(strip)
-                for strip in run_of(s + 2):
-                    widen(strip, False)
-            else:
-                catch_up_r(s + 1)
-                if unit == 1:
-                    quant_f(NT - 1)
-                if unit == 3:
-                    leaky(2 * NPAIR - 1, nc.vector, 0, 2 * QW)
-        finish(units - 1)
+            if unit == 1:
+                finish(0, nc.vector, left_of(0))
+                quant_f(NT - 1)
+            react(unit + 1)
+            catch_up_r(s + 1)
+            finish(unit, nc.vector, left_of(unit))
+            finish(unit + 1, nc.gpsimd, gained[unit % NGAINED][:])
+        react(PAIRED_END)
+        for unit in range(PAIRED_END + 1, units):
+            react(unit)
+            finish(unit - 1, nc.vector, left_of(unit - 1))
+        finish(units - 1, nc.vector, left_of(units - 1))

@@ -28,12 +28,14 @@ QW = 256
 NQ = A // QW
 NPAIR = NT // 2
 NRU = (A // P) * (L // SPAN)
-HEAD_C = 3
+HEAD_C = 4
+C_LEAD = 3
 C_LOADS = ((0, 1), (1, 5), (5, 8))
+AHEAD = 4
 NGAINED = 6
-PAIRED_END = 11
-SHARED_F = NT - 4
-FIRST_SHARED = 3
+PAIRED_END = 13
+SHARED_F = NT - 3
+SHARED_C = 3
 
 
 def tile_leaky_slope_reconstructor_d6_kernel(
@@ -54,12 +56,13 @@ def tile_leaky_slope_reconstructor_d6_kernel(
         g_sc = tiles("g_sc", 1, [P, GA, L], U8)[0]
         r_raw = tiles("r_raw", 2 * NQ, [P, 2, SPAN], U8)
         r_sc = tiles("r_sc", 1, [P, (A // P) * (L // P)], F32)[0]
-        s_sb = tiles("s_sb", NT, [P, L], BF16)
+        s_sb = tiles("s_sb", 2 * NT, [P, SPAN], BF16)
         prev_sb = tiles("prev_sb", 2 * NPAIR, [P, 2, 2 * QW], BF16)
         gain_sb = tiles("gain_sb", 1, [P, A], BF16)[0]
         leak_sb = tiles("leak_sb", 1, [P, A], BF16)[0]
         ident = tiles("ident", 1, [P, P], F32)[0]
-        wide = tiles("wide", 8, [P, SPAN], BF16)
+        wide = tiles("wide", 6, [P, SPAN], BF16)
+        wide_head = tiles("wide_head", HEAD_C, [P, SPAN], BF16)
         c_codes = tiles("c_codes", 3, [P, GA * P], U32)
         c_planes = tiles("c_planes", 3, [P, GA * P], U8)
         r_four = tiles("r_four", 2, [P, 2, QW, 4], BF16)
@@ -70,7 +73,7 @@ def tile_leaky_slope_reconstructor_d6_kernel(
         f_codes = tiles("f_codes", NT, [P, GL * P], U32)
         f_planes = tiles("f_planes", NT, [P, GL * P], U8)
         left = tiles("left", 2 * NPAIR, [P, 2, 2 * QW], F32)
-        c_head = tiles("c_head", FIRST_SHARED, [P, 2 * QW], F32)
+        c_ring = tiles("c_ring", 3, [P, 2 * QW], F32)
         gained = tiles("gained", NGAINED, [P, 2, QW], F32)
         acc = [psum.tile([P, 512], F32, name="acc%d" % k) for k in range(4)]
         turn_bank = [psum.tile([P, 2, 2, P], F32, name="turn%d" % k) for k in range(4)]
@@ -89,8 +92,12 @@ def tile_leaky_slope_reconstructor_d6_kernel(
         def load_g(n):
             nc.sync.dma_start(out=g_words[n][:].bitcast(I32), in_=g_v[:, :, L * n : L * (n + 1)].bitcast(I32))
 
+        def load_s_half(i, h):
+            nc.sync.dma_start(out=s_sb[2 * i + h][:], in_=s_v[:, i, SPAN * h : SPAN * (h + 1)])
+
         def load_s(i):
-            nc.sync.dma_start(out=s_sb[i][:], in_=s_v[:, i, :])
+            load_s_half(i, 0)
+            load_s_half(i, 1)
 
         def load_r(h):
             q, half = h // 2, h % 2
@@ -112,20 +119,21 @@ def tile_leaky_slope_reconstructor_d6_kernel(
                 in_=G_scales[:, 4 * q : 4 * q + 4, :].rearrange("g q n -> q g n").bitcast(I32),
             )
         load_g(1)
-        load_s(0)
+        load_s_half(0, 0)
         nc.sync.dma_start(out=r_sc[:], in_=R_scale.rearrange("i j -> (i j)").partition_broadcast(P))
         load_r(0)
+        load_s_half(0, 1)
         load_s(1)
         load_c(2)
         nc.sync.dma_start(out=leak_sb[:], in_=leak.partition_broadcast(P))
         for s in range(2, NT):
             load_prev(s - 2)
             load_s(s)
-            if s in (2, 3):
-                load_prev(NT - 4 + s)
             load_r(s - 1)
         nc.sync.dma_start(out=gain_sb[:], in_=gain.partition_broadcast(P))
         load_r(NT - 1)
+        load_prev(NT - 2)
+        load_prev(NT - 1)
 
         order = {}
 
@@ -139,9 +147,12 @@ def tile_leaky_slope_reconstructor_d6_kernel(
             return r_raw[k // 2][:, row, :], r_sc[:, first : first + SPAN // P]
 
         def widen(strip, on_vector):
-            order[strip] = len(order)
+            if on_vector:
+                order[strip] = wide_head[strip[1]]
+            else:
+                order[strip] = wide[(len(order) - HEAD_C) % len(wide)]
             raw, scale = strip_source(strip)
-            dst = wide[order[strip] % len(wide)]
+            dst = order[strip]
             for j in range(SPAN // P):
                 k = slice(P * j, P * (j + 1))
                 if on_vector:
@@ -152,11 +163,11 @@ def tile_leaky_slope_reconstructor_d6_kernel(
                     nc.scalar.activation(out=dst[:, k], in_=raw[:, k].bitcast(FP8), func=COPY, scale=scale[:, j : j + 1])
 
         def c_four(i):
-            room = c_head[i][:] if i < FIRST_SHARED else left[i - FIRST_SHARED][:, 0, :]
+            room = left[0][:, 0, :] if i == SHARED_C else c_ring[i % len(c_ring)][:]
             return room.bitcast(BF16).rearrange("p (g r j) -> p g r j", g=GA, j=4)
 
         def f_four(i):
-            room = left[NT - FIRST_SHARED] if i == SHARED_F else f_ring[i % 2]
+            room = left[i + 1] if i < SHARED_F else f_ring[i % 2]
             return room[:].rearrange("p s a -> p (s a)").bitcast(BF16).rearrange("p (g r j) -> p g r j", g=GL, j=4)
 
         turned = []
@@ -170,7 +181,7 @@ def tile_leaky_slope_reconstructor_d6_kernel(
 
         def turn_strip(strip):
             kind, k = strip
-            words = wide[order[strip] % len(wide)][:].bitcast(F32)
+            words = order[strip][:].bitcast(F32)
             bank = next_bank()
             for g in range(2):
                 for u in range(2):
@@ -209,7 +220,7 @@ def tile_leaky_slope_reconstructor_d6_kernel(
                 nc.vector.tensor_tensor(
                     out=full[(2 * i + n // 2) % 4][:, n % 2, :, :, :],
                     in0=acc[n][:].rearrange("p (w u e) -> p u w e", u=2, e=2),
-                    in1=s_sb[i][:, 512 * n : 512 * (n + 1)].rearrange("p (w u e) -> p u w e", u=2, e=2),
+                    in1=s_sb[2 * i + n // 2][:, 512 * (n % 2) : 512 * (n % 2 + 1)].rearrange("p (w u e) -> p u w e", u=2, e=2),
                     op=ADD,
                 )
 
@@ -263,7 +274,7 @@ def tile_leaky_slope_reconstructor_d6_kernel(
         runs = []
         taken = 0
         for s in range(NT):
-            run = [("c", s + HEAD_C)] if s + HEAD_C < NT else []
+            run = [("c", i) for i in range(HEAD_C, NT) if s == (0 if i == HEAD_C else i - C_LEAD)]
             while len(run) < 1 + s % 2:
                 run.append(("r", taken))
                 taken = taken + 1
@@ -278,15 +289,24 @@ def tile_leaky_slope_reconstructor_d6_kernel(
         def ready_halves(s):
             return sum(1 for r in runs[:s] for kind, k in r if kind == "r") // 2
 
+        waiting = [strip for run in runs for strip in run]
+
+        def widen_ahead(s):
+            target = sum(len(run) for run in runs[: s + 1]) + AHEAD
+            for strip in waiting[len(order) - HEAD_C : target]:
+                widen(strip, False)
+
         widen(("c", 0), True)
         turn_strip(("c", 0))
         widen(("c", 1), True)
         widen(("c", 2), True)
         quant_c(0)
         widen(("c", 3), True)
-        turn_strip(("c", 1))
-        turn_strip(("c", 2))
+        for i in range(1, HEAD_C):
+            turn_strip(("c", i))
         quant_c(1)
+        for strip in waiting[:3]:
+            widen(strip, False)
 
         units = NQ * NPAIR
         quantized = []
@@ -298,26 +318,23 @@ def tile_leaky_slope_reconstructor_d6_kernel(
 
         for s in range(NT):
             mirror(s)
-            if s == 0:
-                for strip in run_of(1):
-                    widen(strip, False)
-            catch_up_r(s)
-            if 3 <= s <= 6:
-                leaky(NT - 2 + (s - 3) // 2, nc.vector, QW * ((s - 3) % 2), QW * ((s - 3) % 2 + 1))
+            if s + 2 < NT:
+                catch_up_r(s)
             if s >= 2:
                 quant_f(s - 2)
-            if s - 2 == SHARED_F:
-                leaky(NT - FIRST_SHARED, nc.gpsimd, 0, 2 * QW)
             if s + 2 < NT:
                 quant_c(s + 2)
-                if s + 2 >= FIRST_SHARED:
-                    leaky(s + 2 - FIRST_SHARED, nc.gpsimd, 0, 2 * QW)
+            else:
+                catch_up_r(s)
+            if s + 2 == SHARED_C:
+                leaky(0, nc.gpsimd, 0, 2 * QW)
+            if 0 <= s - 2 < SHARED_F:
+                leaky(s - 1, nc.gpsimd, 0, 2 * QW)
             for strip in run_of(s):
                 turn_strip(strip)
             if s >= 1:
                 turn_f(s - 1)
-            for strip in run_of(s + 2):
-                widen(strip, False)
+            widen_ahead(s)
 
         react(0)
         catch_up_r(NT)
@@ -328,16 +345,21 @@ def tile_leaky_slope_reconstructor_d6_kernel(
                 turn_f(NT - 1)
             for strip in run_of(s):
                 turn_strip(strip)
-            for strip in run_of(s + 2):
-                widen(strip, False)
+            widen_ahead(s)
             react(unit)
             if unit == 1:
                 finish(0, nc.vector, left_of(0))
                 quant_f(NT - 1)
             react(unit + 1)
-            catch_up_r(s + 1)
+            if run_of(s):
+                part = unit // 2
+                leaky(NT - 2 + part % 2, nc.vector, QW * (part // 2), QW * (part // 2 + 1))
             finish(unit, nc.vector, left_of(unit))
-            finish(unit + 1, nc.gpsimd, gained[unit % NGAINED][:])
+            if run_of(s):
+                catch_up_r(s + 1)
+                finish(unit + 1, nc.gpsimd, gained[unit % NGAINED][:])
+            else:
+                finish(unit + 1, nc.gpsimd, left_of(unit + 1))
         react(PAIRED_END)
         for unit in range(PAIRED_END + 1, units):
             react(unit)

@@ -130,10 +130,10 @@ def tile_leaky_slope_reconstructor_d6_kernel(
             load_prev(s - 2)
             load_s(s)
             load_r(s - 1)
+            if s in (2, 3):
+                load_prev(NT - 4 + s)
         nc.sync.dma_start(out=gain_sb[:], in_=gain.partition_broadcast(P))
         load_r(NT - 1)
-        load_prev(NT - 2)
-        load_prev(NT - 1)
 
         order = {}
 
@@ -271,11 +271,15 @@ def tile_leaky_slope_reconstructor_d6_kernel(
             engine.tensor_tensor(out=result, in0=gained[unit % NGAINED][:], in1=left_of(unit), op=ADD)
             nc.sync.dma_start(out=o_v[:, 2 * m : 2 * m + 2, QW * q : QW * (q + 1)], in_=result)
 
+        def warm_up(count):
+            for k in range(count):
+                nc.tensor.matmul(acc[3][:, 0:P], lhsT=ident[:], rhs=ident[:], start=True, stop=True)
+
         runs = []
         taken = 0
         for s in range(NT):
             run = [("c", i) for i in range(HEAD_C, NT) if s == (0 if i == HEAD_C else i - C_LEAD)]
-            while len(run) < 1 + s % 2:
+            while len(run) < 1 + (s % 4 == 1):
                 run.append(("r", taken))
                 taken = taken + 1
             runs.append(run)
@@ -296,6 +300,7 @@ def tile_leaky_slope_reconstructor_d6_kernel(
             for strip in waiting[len(order) - HEAD_C : target]:
                 widen(strip, False)
 
+        warm_up(4)
         widen(("c", 0), True)
         turn_strip(("c", 0))
         widen(("c", 1), True)
@@ -303,7 +308,9 @@ def tile_leaky_slope_reconstructor_d6_kernel(
         quant_c(0)
         widen(("c", 3), True)
         for i in range(1, HEAD_C):
+            warm_up(1)
             turn_strip(("c", i))
+        warm_up(1)
         quant_c(1)
         for strip in waiting[:3]:
             widen(strip, False)
@@ -318,6 +325,8 @@ def tile_leaky_slope_reconstructor_d6_kernel(
 
         for s in range(NT):
             mirror(s)
+            if 3 <= s <= 6:
+                leaky(NT - 2 + (s - 3) // 2, nc.vector, QW * ((s - 3) % 2), QW * ((s - 3) % 2 + 1))
             if s + 2 < NT:
                 catch_up_r(s)
             if s >= 2:
@@ -350,16 +359,10 @@ def tile_leaky_slope_reconstructor_d6_kernel(
             if unit == 1:
                 finish(0, nc.vector, left_of(0))
                 quant_f(NT - 1)
+            catch_up_r(s + 1)
             react(unit + 1)
-            if run_of(s):
-                part = unit // 2
-                leaky(NT - 2 + part % 2, nc.vector, QW * (part // 2), QW * (part // 2 + 1))
             finish(unit, nc.vector, left_of(unit))
-            if run_of(s):
-                catch_up_r(s + 1)
-                finish(unit + 1, nc.gpsimd, gained[unit % NGAINED][:])
-            else:
-                finish(unit + 1, nc.gpsimd, left_of(unit + 1))
+            finish(unit + 1, nc.gpsimd, left_of(unit + 1))
         react(PAIRED_END)
         for unit in range(PAIRED_END + 1, units):
             react(unit)

@@ -60,6 +60,8 @@ def tile_leaky_slope_reconstructor_d6_kernel(
         prev_sb = tiles("prev_sb", 2 * NPAIR, [P, 2, 2 * QW], BF16)
         gain_sb = tiles("gain_sb", 1, [P, A], BF16)[0]
         leak_sb = tiles("leak_sb", 1, [P, A], BF16)[0]
+        r_col = tiles("r_col", 1, [P, 1], F32)[0]
+        leak_col = tiles("leak_col", 1, [P, A // P], BF16)[0]
         ident = tiles("ident", 1, [P, P], F32)[0]
         wide = tiles("wide", 6, [P, SPAN], BF16)
         wide_head = tiles("wide_head", HEAD_C, [P, SPAN], BF16)
@@ -111,6 +113,8 @@ def tile_leaky_slope_reconstructor_d6_kernel(
         make_identity(nc, ident[:])
         nc.sync.dma_start(out=c_sc[:], in_=C_scale.rearrange("(p i) j -> p i j", i=NT))
         load_c(0)
+        nc.sync.dma_start(out=r_col[:], in_=R_scale.rearrange("i (j o) -> (i j) o", o=1))
+        nc.sync.dma_start(out=leak_col[:], in_=leak.rearrange("(p e) -> p e", p=P))
         load_c(1)
         load_g(0)
         for q in range(4):
@@ -120,20 +124,18 @@ def tile_leaky_slope_reconstructor_d6_kernel(
             )
         load_g(1)
         load_s_half(0, 0)
-        nc.sync.dma_start(out=r_sc[:], in_=R_scale.rearrange("i j -> (i j)").partition_broadcast(P))
         load_r(0)
         load_s_half(0, 1)
         load_s(1)
         load_c(2)
-        nc.sync.dma_start(out=leak_sb[:], in_=leak.partition_broadcast(P))
         for s in range(2, NT):
             load_prev(s - 2)
             load_s(s)
             load_r(s - 1)
             if s in (2, 3):
                 load_prev(NT - 4 + s)
-        nc.sync.dma_start(out=gain_sb[:], in_=gain.partition_broadcast(P))
         load_r(NT - 1)
+        nc.sync.dma_start(out=gain_sb[:], in_=gain.partition_broadcast(P))
 
         order = {}
 
@@ -271,6 +273,17 @@ def tile_leaky_slope_reconstructor_d6_kernel(
             engine.tensor_tensor(out=result, in0=gained[unit % NGAINED][:], in1=left_of(unit), op=ADD)
             nc.sync.dma_start(out=o_v[:, 2 * m : 2 * m + 2, QW * q : QW * (q + 1)], in_=result)
 
+        def spread(words, bank):
+            for j in range(words.shape[1]):
+                nc.tensor.transpose(bank[:, P * j : P * (j + 1)], words[:, j : j + 1].to_broadcast([P, P]), ident[:])
+
+        def gather(bank, dst):
+            count = dst.shape[1] // P
+            nc.vector.tensor_copy(
+                out=dst.rearrange("p (n j) -> p n j", j=count),
+                in_=bank[:, : P * count].rearrange("p (j n) -> p n j", j=count),
+            )
+
         def warm_up(count):
             for k in range(count):
                 nc.tensor.matmul(acc[3][:, 0:P], lhsT=ident[:], rhs=ident[:], start=True, stop=True)
@@ -307,11 +320,16 @@ def tile_leaky_slope_reconstructor_d6_kernel(
         widen(("c", 2), True)
         quant_c(0)
         widen(("c", 3), True)
-        for i in range(1, HEAD_C):
+        for i in range(1, HEAD_C - 1):
             warm_up(1)
             turn_strip(("c", i))
+        spread(r_col[:], acc[1])
+        spread(leak_col[:].bitcast(F32), acc[2])
+        turn_strip(("c", HEAD_C - 1))
         warm_up(1)
+        gather(acc[1], r_sc[:])
         quant_c(1)
+        gather(acc[2], leak_sb[:].bitcast(F32))
         for strip in waiting[:3]:
             widen(strip, False)
 

@@ -32,7 +32,7 @@ HEAD_C = 4
 C_LEAD = 3
 C_LOADS = ((0, 1), (1, 5), (5, 8))
 AHEAD = 4
-NGAINED = 6
+NGAINED = 4
 PAIRED_END = 13
 SHARED_F = NT - 3
 SHARED_C = 3
@@ -67,7 +67,7 @@ def tile_leaky_slope_reconstructor_d6_kernel(
         wide_head = tiles("wide_head", HEAD_C, [P, SPAN], BF16)
         c_codes = tiles("c_codes", 3, [P, GA * P], U32)
         c_planes = tiles("c_planes", 3, [P, GA * P], U8)
-        r_four = tiles("r_four", 2, [P, 2, QW, 4], BF16)
+        r_four = tiles("r_four", 3, [P, 2, QW, 4], BF16)
         r_codes = tiles("r_codes", 2 * NQ, [P, 2 * QW], U32)
         r_planes = tiles("r_planes", 2 * NQ, [P, 2 * QW], U8)
         full = tiles("full", 4, [P, 2, 2, P, 2], BF16)
@@ -117,10 +117,10 @@ def tile_leaky_slope_reconstructor_d6_kernel(
         nc.sync.dma_start(out=leak_col[:], in_=leak.rearrange("(p e) -> p e", p=P))
         load_c(1)
         load_g(0)
-        for q in range(4):
+        for r in range(4):
             nc.scalar.dma_start(
-                out=g_sc[32 * q : 32 * q + 4, :, :].bitcast(I32),
-                in_=G_scales[:, 4 * q : 4 * q + 4, :].rearrange("g q n -> q g n").bitcast(I32),
+                out=g_sc[r:P:32, :, :].bitcast(I32),
+                in_=G_scales[:, r:16:4, :].rearrange("g q n -> q g n").bitcast(I32),
             )
         load_g(1)
         load_s_half(0, 0)
@@ -193,7 +193,7 @@ def tile_leaky_slope_reconstructor_d6_kernel(
                 empty(bank, c_four(k))
             else:
                 row = k % 2
-                empty(bank, r_four[(k // 2) % 2][:, :, P * row : P * (row + 1), :])
+                empty(bank, r_four[(k // 2) % 3][:, :, P * row : P * (row + 1), :])
 
         def quantize(codes, planes, four):
             nc.vector.quantize_mx(out=codes[:].bitcast(FP8X4), scales=planes[:], in_=four.rearrange("p g r j -> p (g r j)"))
@@ -202,7 +202,7 @@ def tile_leaky_slope_reconstructor_d6_kernel(
             quantize(c_codes[i % 3], c_planes[i % 3], c_four(i))
 
         def quant_r(h):
-            quantize(r_codes[h], r_planes[h], r_four[h % 2][:])
+            quantize(r_codes[h], r_planes[h], r_four[h % 3][:])
 
         def quant_f(i):
             quantize(f_codes[i], f_planes[i], f_four(i))
@@ -248,10 +248,10 @@ def tile_leaky_slope_reconstructor_d6_kernel(
             q, m = unit // NPAIR, unit % NPAIR
             return left[NPAIR * (q // 2) + m][:, :, QW * (q % 2) : QW * (q % 2 + 1)]
 
-        def react(unit):
+        def react(unit, sides=slice(0, 2), shift=0):
             q, m = unit // NPAIR, unit % NPAIR
-            bank = acc[unit % 4]
-            for side in range(2):
+            bank = acc[(unit + shift) % 4]
+            for side in range(sides.start, sides.stop):
                 i = 2 * m + side
                 for g in range(GL):
                     cols = slice(QW * (g % 2), QW * (g % 2 + 1))
@@ -265,13 +265,16 @@ def tile_leaky_slope_reconstructor_d6_kernel(
                         stop=(g == GL - 1),
                     )
             nc.vector.tensor_tensor(
-                out=gained[unit % NGAINED][:], in0=bank[:].rearrange("p (s a) -> p s a", s=2), in1=along(gain_sb, q), op=MULT
+                out=gained[unit % NGAINED][:, sides, :],
+                in0=bank[:].rearrange("p (s a) -> p s a", s=2)[:, sides, :],
+                in1=along(gain_sb, q)[:, sides, :],
+                op=MULT,
             )
 
-        def finish(unit, engine, result):
+        def finish(unit, engine, result, sides=slice(0, 2)):
             q, m = unit // NPAIR, unit % NPAIR
-            engine.tensor_tensor(out=result, in0=gained[unit % NGAINED][:], in1=left_of(unit), op=ADD)
-            nc.sync.dma_start(out=o_v[:, 2 * m : 2 * m + 2, QW * q : QW * (q + 1)], in_=result)
+            engine.tensor_tensor(out=result[:, sides, :], in0=gained[unit % NGAINED][:, sides, :], in1=left_of(unit)[:, sides, :], op=ADD)
+            nc.sync.dma_start(out=o_v[:, 2 * m : 2 * m + 2, QW * q : QW * (q + 1)][:, sides, :], in_=result[:, sides, :])
 
         def spread(words, bank):
             for j in range(words.shape[1]):
@@ -309,7 +312,7 @@ def tile_leaky_slope_reconstructor_d6_kernel(
         waiting = [strip for run in runs for strip in run]
 
         def widen_ahead(s):
-            target = sum(len(run) for run in runs[: s + 1]) + AHEAD
+            target = sum(len(run) for run in runs[: s + 1]) + (AHEAD if s < NT else AHEAD - 1)
             for strip in waiting[len(order) - HEAD_C : target]:
                 widen(strip, False)
 
@@ -366,6 +369,7 @@ def tile_leaky_slope_reconstructor_d6_kernel(
         react(0)
         catch_up_r(NT)
         quant_f(NT - 2)
+        finish(0, nc.vector, left_of(0))
         for unit in range(1, PAIRED_END, 2):
             s = NT + unit // 2
             if unit == 1:
@@ -375,14 +379,17 @@ def tile_leaky_slope_reconstructor_d6_kernel(
             widen_ahead(s)
             react(unit)
             if unit == 1:
-                finish(0, nc.vector, left_of(0))
                 quant_f(NT - 1)
             catch_up_r(s + 1)
             react(unit + 1)
             finish(unit, nc.vector, left_of(unit))
             finish(unit + 1, nc.gpsimd, left_of(unit + 1))
         react(PAIRED_END)
-        for unit in range(PAIRED_END + 1, units):
-            react(unit)
-            finish(unit - 1, nc.vector, left_of(unit - 1))
-        finish(units - 1, nc.vector, left_of(units - 1))
+        last = units - 1
+        finish(PAIRED_END, nc.gpsimd, left_of(PAIRED_END))
+        react(last - 1)
+        react(last, slice(0, 1))
+        react(last, slice(1, 2), 1)
+        finish(last - 1, nc.vector, left_of(last - 1))
+        finish(last, nc.vector, left_of(last), slice(0, 1))
+        finish(last, nc.vector, left_of(last), slice(1, 2))

@@ -31,6 +31,7 @@ NRU = (A // P) * (L // SPAN)
 HEAD_C = 4
 C_LEAD = 3
 C_LOADS = ((0, 1), (1, 5), (5, 8))
+VECTOR_FROM = 8
 AHEAD = 4
 NGAINED = 4
 PAIRED_END = 13
@@ -178,8 +179,9 @@ def tile_leaky_slope_reconstructor_d6_kernel(
             turned.append(len(turned))
             return turn_bank[turned[-1] % len(turn_bank)]
 
-        def empty(bank, dst):
-            nc.scalar.copy(out=dst.bitcast(F32), in_=bank[:].rearrange("p g u r -> p g r u"))
+        def empty(bank, dst, on_vector=False):
+            copy = nc.vector.tensor_copy if on_vector else nc.scalar.copy
+            copy(out=dst.bitcast(F32), in_=bank[:].rearrange("p g u r -> p g r u"))
 
         def turn_strip(strip):
             kind, k = strip
@@ -193,7 +195,7 @@ def tile_leaky_slope_reconstructor_d6_kernel(
                 empty(bank, c_four(k))
             else:
                 row = k % 2
-                empty(bank, r_four[(k // 2) % 3][:, :, P * row : P * (row + 1), :])
+                empty(bank, r_four[(k // 2) % 3][:, :, P * row : P * (row + 1), :], k >= VECTOR_FROM and row == 1)
 
         def quantize(codes, planes, four):
             nc.vector.quantize_mx(out=codes[:].bitcast(FP8X4), scales=planes[:], in_=four.rearrange("p g r j -> p (g r j)"))

@@ -27,14 +27,11 @@ SPAN = 1024
 QW = 256
 NQ = A // QW
 NPAIR = NT // 2
-NRU = (A // P) * (L // SPAN)
+NH = 2 * NQ
 HEAD_C = 4
-C_LEAD = 3
 C_LOADS = ((0, 1), (1, 5), (5, 8))
-VECTOR_FROM = 8
-AHEAD = 4
-NGAINED = 4
-PAIRED_END = 13
+PLAIN = (0, 1, 4, 6)
+NGAINED = 8
 SHARED_F = NT - 3
 SHARED_C = 3
 
@@ -55,20 +52,19 @@ def tile_leaky_slope_reconstructor_d6_kernel(
         c_sc = tiles("c_sc", 1, [P, NT, A // P], F32)[0]
         g_words = tiles("g_words", NL // 2, [P, GA, L], U8)
         g_sc = tiles("g_sc", 1, [P, GA, L], U8)[0]
-        r_raw = tiles("r_raw", 2 * NQ, [P, 2, SPAN], U8)
-        r_sc = tiles("r_sc", 1, [P, (A // P) * (L // P)], F32)[0]
-        s_sb = tiles("s_sb", 2 * NT, [P, SPAN], BF16)
+        r_raw = tiles("r_raw", NH, [P, L], U8)
+        r_sc = tiles("r_sc", 1, [P, NQ, L // P], F32)[0]
+        s_sb = tiles("s_sb", NT, [P, L], BF16)
         prev_sb = tiles("prev_sb", 2 * NPAIR, [P, 2, 2 * QW], BF16)
         gain_sb = tiles("gain_sb", 1, [P, A], BF16)[0]
         leak_sb = tiles("leak_sb", 1, [P, A], BF16)[0]
         r_col = tiles("r_col", 1, [P, 1], F32)[0]
         leak_col = tiles("leak_col", 1, [P, A // P], BF16)[0]
         ident = tiles("ident", 1, [P, P], F32)[0]
-        wide = tiles("wide", 6, [P, SPAN], BF16)
-        wide_head = tiles("wide_head", HEAD_C, [P, SPAN], BF16)
+        wide = tiles("wide", 4, [P, 2 * SPAN], BF16)
+        r_cast = tiles("r_cast", 2, [P, 2 * SPAN], BF16)
         c_codes = tiles("c_codes", 3, [P, GA * P], U32)
         c_planes = tiles("c_planes", 3, [P, GA * P], U8)
-        r_four = tiles("r_four", 3, [P, 2, QW, 4], BF16)
         r_codes = tiles("r_codes", 2 * NQ, [P, 2 * QW], U32)
         r_planes = tiles("r_planes", 2 * NQ, [P, 2 * QW], U8)
         full = tiles("full", 4, [P, 2, 2, P, 2], BF16)
@@ -85,7 +81,7 @@ def tile_leaky_slope_reconstructor_d6_kernel(
         s_v = slopes.rearrange("(p i) l -> p i l", i=NT)
         p_v = prev.rearrange("(p i) a -> p i a", i=NT)
         o_v = out.rearrange("(p i) a -> p i a", i=NT)
-        r_v = R_bytes.rearrange("(i p) l -> p i l", p=P)
+        r_v = R_bytes.rearrange("(q p r) l -> q p r l", p=P, r=2)
         g_v = G_words.rearrange("g p n -> p g n")
 
         def load_c(m):
@@ -96,15 +92,24 @@ def tile_leaky_slope_reconstructor_d6_kernel(
             nc.sync.dma_start(out=g_words[n][:].bitcast(I32), in_=g_v[:, :, L * n : L * (n + 1)].bitcast(I32))
 
         def load_s_half(i, h):
-            nc.sync.dma_start(out=s_sb[2 * i + h][:], in_=s_v[:, i, SPAN * h : SPAN * (h + 1)])
+            nc.sync.dma_start(out=s_sb[i][:, SPAN * h : SPAN * (h + 1)], in_=s_v[:, i, SPAN * h : SPAN * (h + 1)])
 
         def load_s(i):
-            load_s_half(i, 0)
-            load_s_half(i, 1)
+            nc.sync.dma_start(out=s_sb[i][:], in_=s_v[:, i, :])
+
+        def raw_r(h):
+            return r_raw[h][:]
 
         def load_r(h):
-            q, half = h // 2, h % 2
-            nc.sync.dma_start(out=r_raw[h][:], in_=r_v[:, 2 * q : 2 * q + 2, SPAN * half : SPAN * (half + 1)])
+            rows = r_v[h // 2][:, :, SPAN * (h % 2) : SPAN * (h % 2 + 1)]
+            if h in PLAIN:
+                nc.sync.dma_start(out=raw_r(h).rearrange("p (r k) -> p r k", r=2), in_=rows)
+            else:
+                for r in range(2):
+                    nc.sync.dma_start(
+                        out=raw_r(h).rearrange("p (j r k) -> p r j k", r=2, k=P)[:, r, :, :],
+                        in_=rows[:, r, :].rearrange("p (j k) -> p j k", k=P),
+                    )
 
         def load_prev(k):
             half, m = k // NPAIR, k % NPAIR
@@ -128,34 +133,31 @@ def tile_leaky_slope_reconstructor_d6_kernel(
         load_r(0)
         load_s_half(0, 1)
         load_s(1)
+        load_prev(0)
         load_c(2)
-        for s in range(2, NT):
-            load_prev(s - 2)
+        load_prev(7)
+        load_prev(1)
+        load_s(2)
+        load_r(1)
+        for s in range(3, NT):
+            load_prev(s - 1)
             load_s(s)
             load_r(s - 1)
-            if s in (2, 3):
-                load_prev(NT - 4 + s)
-        load_r(NT - 1)
+        load_r(7)
         nc.sync.dma_start(out=gain_sb[:], in_=gain.partition_broadcast(P))
 
-        order = {}
+        room_of = {}
 
-        def strip_source(strip):
-            kind, k = strip
-            if kind == "c":
-                m = sum(1 for first, end in C_LOADS if end <= k)
-                return c_raw[m][:, k - C_LOADS[m][0], :], c_sc[:, k, :]
-            q, half, row = k // 4, (k // 2) % 2, k % 2
-            first = (2 * q + row) * (L // P) + half * (SPAN // P)
-            return r_raw[k // 2][:, row, :], r_sc[:, first : first + SPAN // P]
+        def wide_c(i):
+            key = ("c", i // 2)
+            room_of.setdefault(key, wide[len(room_of) % len(wide)])
+            return room_of[key][:, A * (i % 2) : A * (i % 2 + 1)]
 
-        def widen(strip, on_vector):
-            if on_vector:
-                order[strip] = wide_head[strip[1]]
-            else:
-                order[strip] = wide[(len(order) - HEAD_C) % len(wide)]
-            raw, scale = strip_source(strip)
-            dst = order[strip]
+        def wide_r(h):
+            room_of.setdefault(("r", h), wide[len(room_of) % len(wide)])
+            return room_of[("r", h)]
+
+        def widen_row(dst, raw, scale, on_vector):
             for j in range(SPAN // P):
                 k = slice(P * j, P * (j + 1))
                 if on_vector:
@@ -165,12 +167,38 @@ def tile_leaky_slope_reconstructor_d6_kernel(
                 else:
                     nc.scalar.activation(out=dst[:, k], in_=raw[:, k].bitcast(FP8), func=COPY, scale=scale[:, j : j + 1])
 
+        def widen_c(i, on_vector):
+            m = sum(1 for first, end in C_LOADS if end <= i)
+            widen_row(wide_c(i), c_raw[m][:, i - C_LOADS[m][0], :], c_sc[:, i, :], on_vector)
+
+        def r_scales(h):
+            first = (SPAN // P) * (h % 2)
+            return r_sc[:, h // 2, first : first + SPAN // P]
+
+        def widen_r(h, r):
+            row = slice(SPAN * r, SPAN * (r + 1))
+            widen_row(wide_r(h)[:, row], raw_r(h)[:, row], r_scales(h), False)
+
+        def cast_of(h):
+            return r_cast[sum(1 for k in range(h) if k not in PLAIN) % 2]
+
+        def cast_r(h):
+            nc.scalar.copy(out=cast_of(h)[:], in_=raw_r(h).bitcast(FP8))
+
+        def scale_r(h):
+            src = cast_of(h)[:].rearrange("p (j r w u e) -> p j u r w e", r=2, w=32, u=2, e=2)
+            dst = wide_r(h)[:].rearrange("p (g u r b w e) -> p g b u r w e", g=2, u=2, r=2, b=4, e=2)
+            for j in range(SPAN // P):
+                nc.vector.tensor_scalar(
+                    out=dst[:, j // 4, j % 4], in0=src[:, j], scalar1=r_scales(h)[:, j : j + 1], scalar2=None, op0=MULT
+                )
+
         def c_four(i):
-            room = left[0][:, 0, :] if i == SHARED_C else c_ring[i % len(c_ring)][:]
+            room = left[i - 2][:, 0, :] if i in (2, 3) else c_ring[i % len(c_ring)][:]
             return room.bitcast(BF16).rearrange("p (g r j) -> p g r j", g=GA, j=4)
 
         def f_four(i):
-            room = left[i + 1] if i < SHARED_F else f_ring[i % 2]
+            room = left[i + 2] if i < SHARED_F else f_ring[i % 2]
             return room[:].rearrange("p s a -> p (s a)").bitcast(BF16).rearrange("p (g r j) -> p g r j", g=GL, j=4)
 
         turned = []
@@ -179,23 +207,36 @@ def tile_leaky_slope_reconstructor_d6_kernel(
             turned.append(len(turned))
             return turn_bank[turned[-1] % len(turn_bank)]
 
-        def empty(bank, dst, on_vector=False):
-            copy = nc.vector.tensor_copy if on_vector else nc.scalar.copy
-            copy(out=dst.bitcast(F32), in_=bank[:].rearrange("p g u r -> p g r u"))
-
-        def turn_strip(strip):
-            kind, k = strip
-            words = order[strip][:].bitcast(F32)
+        def turn_c(i):
+            words = wide_c(i).bitcast(F32)
             bank = next_bank()
             for g in range(2):
                 for u in range(2):
                     w0 = 256 * g + u
                     nc.tensor.transpose(bank[:, g, u, :], words[:, w0 : w0 + 255 : 2], ident[:])
-            if kind == "c":
-                empty(bank, c_four(k))
-            else:
-                row = k % 2
-                empty(bank, r_four[(k // 2) % 3][:, :, P * row : P * (row + 1), :], k >= VECTOR_FROM and row == 1)
+            empty(bank, c_four(i))
+
+        def empty(bank, dst):
+            nc.scalar.copy(out=dst.bitcast(F32), in_=bank[:].rearrange("p g u r -> p g r u"))
+
+        def r_four(h):
+            return s_sb[h][:].rearrange("p (g r j) -> p g r j", g=2, j=4)
+
+        def turn_r(h, g):
+            words = wide_r(h)[:].bitcast(F32)
+            bank = next_bank()
+            for r in range(2):
+                for u in range(2):
+                    if h in PLAIN:
+                        w0 = 512 * r + 256 * g + u
+                        nc.tensor.transpose(bank[:, r, u, :], words[:, w0 : w0 + 255 : 2], ident[:])
+                    else:
+                        w0 = P * (4 * g + 2 * u + r)
+                        nc.tensor.transpose(bank[:, r, u, :], words[:, w0 : w0 + P], ident[:])
+            nc.scalar.copy(
+                out=r_four(h)[:, g].bitcast(F32).rearrange("p (a r) u -> p a r u", r=2),
+                in_=bank[:].rearrange("p r u a -> p a r u"),
+            )
 
         def quantize(codes, planes, four):
             nc.vector.quantize_mx(out=codes[:].bitcast(FP8X4), scales=planes[:], in_=four.rearrange("p g r j -> p (g r j)"))
@@ -204,7 +245,7 @@ def tile_leaky_slope_reconstructor_d6_kernel(
             quantize(c_codes[i % 3], c_planes[i % 3], c_four(i))
 
         def quant_r(h):
-            quantize(r_codes[h], r_planes[h], r_four[h % 3][:])
+            quantize(r_codes[h], r_planes[h], r_four(h))
 
         def quant_f(i):
             quantize(f_codes[i], f_planes[i], f_four(i))
@@ -224,7 +265,7 @@ def tile_leaky_slope_reconstructor_d6_kernel(
                 nc.vector.tensor_tensor(
                     out=full[(2 * i + n // 2) % 4][:, n % 2, :, :, :],
                     in0=acc[n][:].rearrange("p (w u e) -> p u w e", u=2, e=2),
-                    in1=s_sb[2 * i + n // 2][:, 512 * (n % 2) : 512 * (n % 2 + 1)].rearrange("p (w u e) -> p u w e", u=2, e=2),
+                    in1=s_sb[i][:, 512 * n : 512 * (n + 1)].rearrange("p (w u e) -> p u w e", u=2, e=2),
                     op=ADD,
                 )
 
@@ -266,6 +307,10 @@ def tile_leaky_slope_reconstructor_d6_kernel(
                         start=(g == 0),
                         stop=(g == GL - 1),
                     )
+
+        def weigh(unit, sides=slice(0, 2), shift=0):
+            q = unit // NPAIR
+            bank = acc[(unit + shift) % 4]
             nc.vector.tensor_tensor(
                 out=gained[unit % NGAINED][:, sides, :],
                 in0=bank[:].rearrange("p (s a) -> p s a", s=2)[:, sides, :],
@@ -273,10 +318,16 @@ def tile_leaky_slope_reconstructor_d6_kernel(
                 op=MULT,
             )
 
+        stores = []
+
         def finish(unit, engine, result, sides=slice(0, 2)):
             q, m = unit // NPAIR, unit % NPAIR
             engine.tensor_tensor(out=result[:, sides, :], in0=gained[unit % NGAINED][:, sides, :], in1=left_of(unit)[:, sides, :], op=ADD)
-            nc.sync.dma_start(out=o_v[:, 2 * m : 2 * m + 2, QW * q : QW * (q + 1)][:, sides, :], in_=result[:, sides, :])
+            stores.append((o_v[:, 2 * m : 2 * m + 2, QW * q : QW * (q + 1)][:, sides, :], result[:, sides, :]))
+            if engine is nc.vector:
+                for dst, src in reversed(stores):
+                    nc.sync.dma_start(out=dst, in_=src)
+                stores.clear()
 
         def spread(words, bank):
             for j in range(words.shape[1]):
@@ -293,105 +344,149 @@ def tile_leaky_slope_reconstructor_d6_kernel(
             for k in range(count):
                 nc.tensor.matmul(acc[3][:, 0:P], lhsT=ident[:], rhs=ident[:], start=True, stop=True)
 
-        runs = []
-        taken = 0
-        for s in range(NT):
-            run = [("c", i) for i in range(HEAD_C, NT) if s == (0 if i == HEAD_C else i - C_LEAD)]
-            while len(run) < 1 + (s % 4 == 1):
-                run.append(("r", taken))
-                taken = taken + 1
-            runs.append(run)
-        while taken < NRU:
-            runs.append([("r", k) for k in range(taken, min(taken + 2, NRU))])
-            taken = taken + 2
-
-        def run_of(s):
-            return runs[s] if s < len(runs) else []
-
-        def ready_halves(s):
-            return sum(1 for r in runs[:s] for kind, k in r if kind == "r") // 2
-
-        waiting = [strip for run in runs for strip in run]
-
-        def widen_ahead(s):
-            target = sum(len(run) for run in runs[: s + 1]) + (AHEAD if s < NT else AHEAD - 1)
-            for strip in waiting[len(order) - HEAD_C : target]:
-                widen(strip, False)
+        def spare(room):
+            return room[:].bitcast(F32)[:, : 2 * QW].rearrange("p (s a) -> p s a", s=2)
 
         warm_up(4)
-        widen(("c", 0), True)
-        turn_strip(("c", 0))
-        widen(("c", 1), True)
-        widen(("c", 2), True)
+        widen_c(0, True)
+        turn_c(0)
+        widen_c(1, True)
+        widen_c(2, True)
         quant_c(0)
-        widen(("c", 3), True)
+        widen_c(3, True)
         for i in range(1, HEAD_C - 1):
             warm_up(1)
-            turn_strip(("c", i))
+            turn_c(i)
         spread(r_col[:], acc[1])
         spread(leak_col[:].bitcast(F32), acc[2])
-        turn_strip(("c", HEAD_C - 1))
+        turn_c(HEAD_C - 1)
         warm_up(1)
-        gather(acc[1], r_sc[:])
+        for side in range(2):
+            part = slice(64 * side, 64 * (side + 1))
+            nc.vector.tensor_copy(
+                out=r_sc[part], in_=acc[1][part, 0:P].rearrange("p (q s j) -> p q s j", s=2, j=L // P)[:, :, side, :]
+            )
         quant_c(1)
         gather(acc[2], leak_sb[:].bitcast(F32))
-        for strip in waiting[:3]:
-            widen(strip, False)
 
-        units = NQ * NPAIR
-        quantized = []
-
-        def catch_up_r(s):
-            while len(quantized) < ready_halves(s):
-                quant_r(len(quantized))
-                quantized.append(s)
+        turns = [[("c", 4)], [("r", 0, 0), ("r", 0, 1)], [("c", 5)], [("c", 6)], [("c", 7)], [("r", 1, 0), ("r", 1, 1)], [("r", 2, 0)], [("r", 2, 1)]]
+        widens = [[("c", 5)], [("c", 6)], [("c", 7)], [("r", 1, 0), ("r", 1, 1)], [("x", 2)], [("x", 3)], [("x", 5)], []]
+        widen_c(4, False)
+        widen_r(0, 0)
+        widen_r(0, 1)
 
         for s in range(NT):
             mirror(s)
-            if 3 <= s <= 6:
-                leaky(NT - 2 + (s - 3) // 2, nc.vector, QW * ((s - 3) % 2), QW * ((s - 3) % 2 + 1))
-            if s + 2 < NT:
-                catch_up_r(s)
-            if s >= 2:
+            if s == 1:
+                leaky(7, nc.vector, 0, 2 * QW)
+            if s == 2:
+                quant_r(0)
+            if s in (5, 6):
+                scale_r(s - 3)
+            if 2 <= s < 7:
                 quant_f(s - 2)
             if s + 2 < NT:
                 quant_c(s + 2)
-            else:
-                catch_up_r(s)
-            if s + 2 == SHARED_C:
-                leaky(0, nc.gpsimd, 0, 2 * QW)
-            if 0 <= s - 2 < SHARED_F:
-                leaky(s - 1, nc.gpsimd, 0, 2 * QW)
-            for strip in run_of(s):
-                turn_strip(strip)
+            if s == 6:
+                quant_r(1)
+            if s < 7:
+                leaky(s, nc.gpsimd, 0, 2 * QW)
+            for job in turns[s]:
+                if job[0] == "c":
+                    turn_c(job[1])
+                else:
+                    turn_r(job[1], job[2])
             if s >= 1:
                 turn_f(s - 1)
-            widen_ahead(s)
+            for job in widens[s]:
+                if job[0] == "c":
+                    widen_c(job[1], False)
+                elif job[0] == "r":
+                    widen_r(job[1], job[2])
+                else:
+                    cast_r(job[1])
+
+        def both(h):
+            turn_r(h, 0)
+            turn_r(h, 1)
+
+        def add_v(unit):
+            finish(unit, nc.vector, left_of(unit))
+
+        def add_g(unit, room):
+            finish(unit, nc.gpsimd, room)
 
         react(0)
-        catch_up_r(NT)
-        quant_f(NT - 2)
-        finish(0, nc.vector, left_of(0))
-        for unit in range(1, PAIRED_END, 2):
-            s = NT + unit // 2
-            if unit == 1:
-                turn_f(NT - 1)
-            for strip in run_of(s):
-                turn_strip(strip)
-            widen_ahead(s)
-            react(unit)
-            if unit == 1:
-                quant_f(NT - 1)
-            catch_up_r(s + 1)
-            react(unit + 1)
-            finish(unit, nc.vector, left_of(unit))
-            finish(unit + 1, nc.gpsimd, left_of(unit + 1))
-        react(PAIRED_END)
-        last = units - 1
-        finish(PAIRED_END, nc.gpsimd, left_of(PAIRED_END))
-        react(last - 1)
+        quant_f(5)
+        quant_r(2)
+        weigh(0)
+        turn_f(NT - 1)
+        both(3)
+        widen_r(4, 0)
+        widen_r(4, 1)
+        cast_r(7)
+        react(1)
+        react(2)
+        quant_f(6)
+        quant_f(7)
+        scale_r(5)
+        add_g(0, spare(cast_of(5)[:, SPAN:]))
+        quant_r(3)
+        react(3)
+        weigh(1)
+        weigh(2)
+        react(4)
+        both(4)
+        both(5)
+        widen_r(6, 0)
+        widen_r(6, 1)
+        add_v(1)
+        add_g(2, gained[1])
+        weigh(3)
+        weigh(4)
+        react(5)
+        react(6)
+        react(7)
+        scale_r(7)
+        add_v(3)
+        quant_r(4)
+        add_g(4, spare(s_sb[4]))
+        quant_r(5)
+        react(8)
+        weigh(5)
+        weigh(6)
+        both(7)
+        both(6)
+        add_v(5)
+        add_g(6, gained[5])
+        weigh(7)
+        weigh(8)
+        react(9)
+        react(10)
+        react(11)
+        add_v(7)
+        quant_r(7)
+        weigh(9)
+        quant_r(6)
+        add_g(8, spare(s_sb[6]))
+        add_v(9)
+        react(12)
+        react(13)
+        weigh(10)
+        weigh(11)
+        react(14)
+        add_g(11, left_of(11))
+        add_v(10)
+        last = 15
         react(last, slice(0, 1))
+        weigh(12)
         react(last, slice(1, 2), 1)
-        finish(last - 1, nc.vector, left_of(last - 1))
+        weigh(13)
+        add_g(13, left_of(13))
+        add_v(12)
+        weigh(14)
+        weigh(last, slice(0, 1))
+        weigh(last, slice(1, 2), 1)
+        add_v(14)
         finish(last, nc.vector, left_of(last), slice(0, 1))
         finish(last, nc.vector, left_of(last), slice(1, 2))

@@ -30,8 +30,9 @@ NPAIR = NT // 2
 NH = 2 * NQ
 HEAD_C = 4
 C_LOADS = ((0, 1), (1, 5), (5, 8))
-PLAIN = (0, 1, 4, 6)
+PLAIN = (0, 2, 4, 6)
 NGAINED = 8
+REVERSE_FROM = 3
 SHARED_F = NT - 3
 SHARED_C = 3
 
@@ -62,7 +63,7 @@ def tile_leaky_slope_reconstructor_d6_kernel(
         leak_col = tiles("leak_col", 1, [P, A // P], BF16)[0]
         ident = tiles("ident", 1, [P, P], F32)[0]
         wide = tiles("wide", 4, [P, 2 * SPAN], BF16)
-        r_cast = tiles("r_cast", 2, [P, 2 * SPAN], BF16)
+        r_plain = tiles("r_plain", 2, [P, 2 * SPAN], BF16)
         c_codes = tiles("c_codes", 3, [P, GA * P], U32)
         c_planes = tiles("c_planes", 3, [P, GA * P], U8)
         r_codes = tiles("r_codes", 2 * NQ, [P, 2 * QW], U32)
@@ -102,14 +103,7 @@ def tile_leaky_slope_reconstructor_d6_kernel(
 
         def load_r(h):
             rows = r_v[h // 2][:, :, SPAN * (h % 2) : SPAN * (h % 2 + 1)]
-            if h in PLAIN:
-                nc.sync.dma_start(out=raw_r(h).rearrange("p (r k) -> p r k", r=2), in_=rows)
-            else:
-                for r in range(2):
-                    nc.sync.dma_start(
-                        out=raw_r(h).rearrange("p (j r k) -> p r j k", r=2, k=P)[:, r, :, :],
-                        in_=rows[:, r, :].rearrange("p (j k) -> p j k", k=P),
-                    )
+            nc.sync.dma_start(out=raw_r(h).rearrange("p (r k) -> p r k", r=2), in_=rows)
 
         def load_prev(k):
             half, m = k // NPAIR, k % NPAIR
@@ -177,20 +171,20 @@ def tile_leaky_slope_reconstructor_d6_kernel(
 
         def widen_r(h, r):
             row = slice(SPAN * r, SPAN * (r + 1))
-            widen_row(wide_r(h)[:, row], raw_r(h)[:, row], r_scales(h), False)
+            room = wide_r(h) if h in PLAIN else r_plain[(h // 2) % 2]
+            widen_row(room[:, row], raw_r(h)[:, row], r_scales(h), False)
 
-        def cast_of(h):
-            return r_cast[sum(1 for k in range(h) if k not in PLAIN) % 2]
+        def reorder_r(h, rows=slice(0, 2)):
+            src = r_plain[(h // 2) % 2][:].bitcast(F32).rearrange("p (r x u j) -> p u r x j", r=2, u=2, j=8)
+            dst = wide_r(h)[:].bitcast(F32).rearrange("p (u r x j) -> p u r x j", r=2, u=2, j=8)
+            nc.vector.tensor_copy(out=dst[:, :, rows], in_=src[:, :, rows])
 
-        def cast_r(h):
-            nc.scalar.copy(out=cast_of(h)[:], in_=raw_r(h).bitcast(FP8))
-
-        def scale_r(h):
-            src = cast_of(h)[:].rearrange("p (j r w u e) -> p j u r w e", r=2, w=32, u=2, e=2)
-            dst = wide_r(h)[:].rearrange("p (g u r b w e) -> p g b u r w e", g=2, u=2, r=2, b=4, e=2)
+        def widen_r_ordered(h, r):
+            dst = wide_r(h)[:].rearrange("p (u r j b i) -> p r j b u i", u=2, r=2, b=4, i=16)
+            src = raw_r(h).rearrange("p (r j b u i) -> p r j b u i", r=2, b=4, u=2, i=16)
             for j in range(SPAN // P):
                 nc.vector.tensor_scalar(
-                    out=dst[:, j // 4, j % 4], in0=src[:, j], scalar1=r_scales(h)[:, j : j + 1], scalar2=None, op0=MULT
+                    out=dst[:, r, j], in0=src[:, r, j].bitcast(FP8), scalar1=r_scales(h)[:, j : j + 1], scalar2=None, op0=MULT
                 )
 
         def c_four(i):
@@ -201,11 +195,19 @@ def tile_leaky_slope_reconstructor_d6_kernel(
             room = left[i + 2] if i < SHARED_F else f_ring[i % 2]
             return room[:].rearrange("p s a -> p (s a)").bitcast(BF16).rearrange("p (g r j) -> p g r j", g=GL, j=4)
 
-        turned = []
+        free_banks = list(turn_bank)
+        filled = []
 
         def next_bank():
-            turned.append(len(turned))
-            return turn_bank[turned[-1] % len(turn_bank)]
+            bank = free_banks[0]
+            free_banks.remove(bank)
+            return bank
+
+        def empty_all():
+            for bank, dst, src in reversed(filled):
+                nc.scalar.copy(out=dst, in_=src)
+                free_banks.append(bank)
+            filled.clear()
 
         def turn_c(i):
             words = wide_c(i).bitcast(F32)
@@ -217,7 +219,7 @@ def tile_leaky_slope_reconstructor_d6_kernel(
             empty(bank, c_four(i))
 
         def empty(bank, dst):
-            nc.scalar.copy(out=dst.bitcast(F32), in_=bank[:].rearrange("p g u r -> p g r u"))
+            filled.append((bank, dst.bitcast(F32), bank[:].rearrange("p g u r -> p g r u")))
 
         def r_four(h):
             return s_sb[h][:].rearrange("p (g r j) -> p g r j", g=2, j=4)
@@ -231,12 +233,9 @@ def tile_leaky_slope_reconstructor_d6_kernel(
                         w0 = 512 * r + 256 * g + u
                         nc.tensor.transpose(bank[:, r, u, :], words[:, w0 : w0 + 255 : 2], ident[:])
                     else:
-                        w0 = P * (4 * g + 2 * u + r)
+                        w0 = P * (4 * u + 2 * r + g)
                         nc.tensor.transpose(bank[:, r, u, :], words[:, w0 : w0 + P], ident[:])
-            nc.scalar.copy(
-                out=r_four(h)[:, g].bitcast(F32).rearrange("p (a r) u -> p a r u", r=2),
-                in_=bank[:].rearrange("p r u a -> p a r u"),
-            )
+            filled.append((bank, r_four(h)[:, g].bitcast(F32).rearrange("p (a r) u -> p a r u", r=2), bank[:].rearrange("p r u a -> p a r u")))
 
         def quantize(codes, planes, four):
             nc.vector.quantize_mx(out=codes[:].bitcast(FP8X4), scales=planes[:], in_=four.rearrange("p g r j -> p (g r j)"))
@@ -262,12 +261,20 @@ def tile_leaky_slope_reconstructor_d6_kernel(
                         start=(g == 0),
                         stop=(g == GA - 1),
                     )
-                nc.vector.tensor_tensor(
-                    out=full[(2 * i + n // 2) % 4][:, n % 2, :, :, :],
-                    in0=acc[n][:].rearrange("p (w u e) -> p u w e", u=2, e=2),
-                    in1=s_sb[i][:, 512 * n : 512 * (n + 1)].rearrange("p (w u e) -> p u w e", u=2, e=2),
-                    op=ADD,
-                )
+                if i < REVERSE_FROM:
+                    add_slopes(i, n)
+                elif n % 2 == 1:
+                    add_slopes(i, n)
+                    add_slopes(i, n - 1)
+
+        def add_slopes(i, n):
+            run = 2 if n < 2 else 16
+            nc.vector.tensor_tensor(
+                out=full[(2 * i + n // 2) % 4][:, n % 2].rearrange("p u w e -> p u (w e)").rearrange("p u (w e) -> p u w e", e=run),
+                in0=acc[n][:].rearrange("p (w u e) -> p u w e", u=2, e=run),
+                in1=s_sb[i][:, 512 * n : 512 * (n + 1)].rearrange("p (w u e) -> p u w e", u=2, e=run),
+                op=ADD,
+            )
 
         def turn_f(i):
             for h in range(2):
@@ -296,7 +303,8 @@ def tile_leaky_slope_reconstructor_d6_kernel(
             bank = acc[(unit + shift) % 4]
             for side in range(sides.start, sides.stop):
                 i = 2 * m + side
-                for g in range(GL):
+                passes = (0, 1, 2, 3) if q < 2 else (2, 3, 0, 1)
+                for g in passes:
                     cols = slice(QW * (g % 2), QW * (g % 2 + 1))
                     nc.tensor.matmul_mx(
                         out=bank[:, QW * side : QW * (side + 1)],
@@ -304,8 +312,8 @@ def tile_leaky_slope_reconstructor_d6_kernel(
                         lhsT_scale=f_planes[i][:, P * g : P * (g + 1)],
                         rhs=r_codes[2 * q + g // 2][:, cols].bitcast(FP8X4),
                         rhs_scale=r_planes[2 * q + g // 2][:, cols],
-                        start=(g == 0),
-                        stop=(g == GL - 1),
+                        start=(g == passes[0]),
+                        stop=(g == passes[-1]),
                     )
 
         def weigh(unit, sides=slice(0, 2), shift=0):
@@ -325,9 +333,12 @@ def tile_leaky_slope_reconstructor_d6_kernel(
             engine.tensor_tensor(out=result[:, sides, :], in0=gained[unit % NGAINED][:, sides, :], in1=left_of(unit)[:, sides, :], op=ADD)
             stores.append((o_v[:, 2 * m : 2 * m + 2, QW * q : QW * (q + 1)][:, sides, :], result[:, sides, :]))
             if engine is nc.vector:
-                for dst, src in reversed(stores):
-                    nc.sync.dma_start(out=dst, in_=src)
-                stores.clear()
+                store()
+
+        def store():
+            for dst, src in reversed(stores):
+                nc.sync.dma_start(out=dst, in_=src)
+            stores.clear()
 
         def spread(words, bank):
             for j in range(words.shape[1]):
@@ -349,7 +360,10 @@ def tile_leaky_slope_reconstructor_d6_kernel(
 
         warm_up(4)
         widen_c(0, True)
+        wide_c(2)
+        widen_c(4, False)
         turn_c(0)
+        empty_all()
         widen_c(1, True)
         widen_c(2, True)
         quant_c(0)
@@ -357,9 +371,11 @@ def tile_leaky_slope_reconstructor_d6_kernel(
         for i in range(1, HEAD_C - 1):
             warm_up(1)
             turn_c(i)
+            empty_all()
         spread(r_col[:], acc[1])
         spread(leak_col[:].bitcast(F32), acc[2])
         turn_c(HEAD_C - 1)
+        empty_all()
         warm_up(1)
         for side in range(2):
             part = slice(64 * side, 64 * (side + 1))
@@ -370,8 +386,7 @@ def tile_leaky_slope_reconstructor_d6_kernel(
         gather(acc[2], leak_sb[:].bitcast(F32))
 
         turns = [[("c", 4)], [("r", 0, 0), ("r", 0, 1)], [("c", 5)], [("c", 6)], [("c", 7)], [("r", 1, 0), ("r", 1, 1)], [("r", 2, 0)], [("r", 2, 1)]]
-        widens = [[("c", 5)], [("c", 6)], [("c", 7)], [("r", 1, 0), ("r", 1, 1)], [("x", 2)], [("x", 3)], [("x", 5)], []]
-        widen_c(4, False)
+        widens = [[("c", 5), ("c", 6)], [("c", 7)], [("r", 1, 0), ("r", 1, 1)], [("r", 2, 0)], [("r", 2, 1), ("r", 3, 0)], [("r", 3, 1)], [("r", 4, 0)], []]
         widen_r(0, 0)
         widen_r(0, 1)
 
@@ -381,8 +396,8 @@ def tile_leaky_slope_reconstructor_d6_kernel(
                 leaky(7, nc.vector, 0, 2 * QW)
             if s == 2:
                 quant_r(0)
-            if s in (5, 6):
-                scale_r(s - 3)
+            if s == 4:
+                reorder_r(1)
             if 2 <= s < 7:
                 quant_f(s - 2)
             if s + 2 < NT:
@@ -398,17 +413,17 @@ def tile_leaky_slope_reconstructor_d6_kernel(
                     turn_r(job[1], job[2])
             if s >= 1:
                 turn_f(s - 1)
+            empty_all()
             for job in widens[s]:
                 if job[0] == "c":
                     widen_c(job[1], False)
-                elif job[0] == "r":
-                    widen_r(job[1], job[2])
                 else:
-                    cast_r(job[1])
+                    widen_r(job[1], job[2])
 
         def both(h):
             turn_r(h, 0)
             turn_r(h, 1)
+            empty_all()
 
         def add_v(unit):
             finish(unit, nc.vector, left_of(unit))
@@ -417,59 +432,65 @@ def tile_leaky_slope_reconstructor_d6_kernel(
             finish(unit, nc.gpsimd, room)
 
         react(0)
+        reorder_r(3)
         quant_f(5)
-        quant_r(2)
         weigh(0)
         turn_f(NT - 1)
+        empty_all()
         both(3)
-        widen_r(4, 0)
         widen_r(4, 1)
-        cast_r(7)
+        widen_r(7, 0)
+        widen_r(7, 1)
         react(1)
         react(2)
         quant_f(6)
+        quant_r(2)
+        widen_r_ordered(5, 0)
+        widen_r_ordered(5, 1)
         quant_f(7)
-        scale_r(5)
-        add_g(0, spare(cast_of(5)[:, SPAN:]))
+        add_g(0, spare(f_ring[1][:].rearrange("p s a -> p (s a)")))
+        store()
         quant_r(3)
         react(3)
-        weigh(1)
-        weigh(2)
         react(4)
-        both(4)
-        both(5)
-        widen_r(6, 0)
-        widen_r(6, 1)
-        add_v(1)
-        add_g(2, gained[1])
+        weigh(1)
+        add_g(1, left_of(1))
+        store()
+        weigh(2)
         weigh(3)
         weigh(4)
+        both(5)
+        both(4)
+        widen_r(6, 0)
+        widen_r(6, 1)
         react(5)
         react(6)
         react(7)
-        scale_r(7)
-        add_v(3)
+        add_v(2)
+        reorder_r(7)
+        quant_r(5)
         quant_r(4)
         add_g(4, spare(s_sb[4]))
-        quant_r(5)
+        add_v(3)
         react(8)
         weigh(5)
+        add_g(5, left_of(5))
+        store()
         weigh(6)
-        both(7)
-        both(6)
-        add_v(5)
-        add_g(6, gained[5])
         weigh(7)
         weigh(8)
+        both(7)
+        both(6)
         react(9)
         react(10)
         react(11)
+        add_v(6)
         add_v(7)
         quant_r(7)
         weigh(9)
         quant_r(6)
-        add_g(8, spare(s_sb[6]))
-        add_v(9)
+        add_g(9, spare(s_sb[6]))
+        add_v(8)
         react(12)
         react(13)
         weigh(10)

@@ -33,6 +33,7 @@ C_LOADS = ((0, 1), (1, 5), (5, 8))
 PLAIN = (0, 2, 4, 6)
 NGAINED = 8
 REVERSE_FROM = 3
+POOL_COLS = 448
 SHARED_F = NT - 3
 SHARED_C = 3
 
@@ -56,7 +57,8 @@ def tile_leaky_slope_reconstructor_d6_kernel(
         r_raw = tiles("r_raw", NH, [P, L], U8)
         r_sc = tiles("r_sc", 1, [P, NQ, L // P], F32)[0]
         s_sb = tiles("s_sb", NT, [P, L], BF16)
-        prev_sb = tiles("prev_sb", 2 * NPAIR, [P, 2, 2 * QW], BF16)
+        prev_all = tiles("prev_all", 1, [P, NT * A], BF16)[0][:].rearrange("p (k s a) -> p k s a", k=NT, s=2)
+        prev_sb = [prev_all[:, k] for k in range(NT)]
         gain_sb = tiles("gain_sb", 1, [P, A], BF16)[0]
         leak_sb = tiles("leak_sb", 1, [P, A], BF16)[0]
         r_col = tiles("r_col", 1, [P, 1], F32)[0]
@@ -72,7 +74,8 @@ def tile_leaky_slope_reconstructor_d6_kernel(
         f_ring = tiles("f_ring", 2, [P, 2, 2 * QW], F32)
         f_codes = tiles("f_codes", NT, [P, GL * P], U32)
         f_planes = tiles("f_planes", NT, [P, GL * P], U8)
-        left = tiles("left", 2 * NPAIR, [P, 2, 2 * QW], F32)
+        left_all = tiles("left_all", 1, [P, NT * A], F32)[0][:].rearrange("p (k s a) -> p k s a", k=NT, s=2)
+        left = [left_all[:, k] for k in range(NT)]
         c_ring = tiles("c_ring", 3, [P, 2 * QW], F32)
         gained = tiles("gained", NGAINED, [P, 2, QW], F32)
         acc = [psum.tile([P, 512], F32, name="acc%d" % k) for k in range(4)]
@@ -151,8 +154,8 @@ def tile_leaky_slope_reconstructor_d6_kernel(
             room_of.setdefault(("r", h), wide[len(room_of) % len(wide)])
             return room_of[("r", h)]
 
-        def widen_row(dst, raw, scale, on_vector):
-            for j in range(SPAN // P):
+        def widen_row(dst, raw, scale, on_vector, blocks=range(SPAN // P)):
+            for j in blocks:
                 k = slice(P * j, P * (j + 1))
                 if on_vector:
                     nc.vector.tensor_scalar(
@@ -161,9 +164,9 @@ def tile_leaky_slope_reconstructor_d6_kernel(
                 else:
                     nc.scalar.activation(out=dst[:, k], in_=raw[:, k].bitcast(FP8), func=COPY, scale=scale[:, j : j + 1])
 
-        def widen_c(i, on_vector):
+        def widen_c(i, on_vector, blocks=range(SPAN // P)):
             m = sum(1 for first, end in C_LOADS if end <= i)
-            widen_row(wide_c(i), c_raw[m][:, i - C_LOADS[m][0], :], c_sc[:, i, :], on_vector)
+            widen_row(wide_c(i), c_raw[m][:, i - C_LOADS[m][0], :], c_sc[:, i, :], on_vector, blocks)
 
         def r_scales(h):
             first = (SPAN // P) * (h % 2)
@@ -294,6 +297,11 @@ def tile_leaky_slope_reconstructor_d6_kernel(
             rates = leak_sb[:, base + first : base + end].unsqueeze(1).to_broadcast([P, 2, end - first])
             engine.tensor_tensor(out=left[k][:, :, first:end], in0=prev_sb[k][:, :, first:end], in1=rates, op=MULT)
 
+        def leaky_rest(first, end):
+            base = 2 * QW * (first // NPAIR)
+            rates = leak_sb[:, base + POOL_COLS : base + 2 * QW].unsqueeze(1).unsqueeze(1).to_broadcast([P, end - first, 2, 2 * QW - POOL_COLS])
+            nc.vector.tensor_tensor(out=left_all[:, first:end, :, POOL_COLS:], in0=prev_all[:, first:end, :, POOL_COLS:], in1=rates, op=MULT)
+
         def left_of(unit):
             q, m = unit // NPAIR, unit % NPAIR
             return left[NPAIR * (q // 2) + m][:, :, QW * (q % 2) : QW * (q % 2 + 1)]
@@ -361,9 +369,9 @@ def tile_leaky_slope_reconstructor_d6_kernel(
         warm_up(4)
         widen_c(0, True)
         wide_c(2)
-        widen_c(4, False)
         turn_c(0)
         empty_all()
+        widen_c(4, False, range(0, 2))
         widen_c(1, True)
         widen_c(2, True)
         quant_c(0)
@@ -372,6 +380,7 @@ def tile_leaky_slope_reconstructor_d6_kernel(
             warm_up(1)
             turn_c(i)
             empty_all()
+            widen_c(4, False, range(2 * i, 4 * i))
         spread(r_col[:], acc[1])
         spread(leak_col[:].bitcast(F32), acc[2])
         turn_c(HEAD_C - 1)
@@ -405,13 +414,15 @@ def tile_leaky_slope_reconstructor_d6_kernel(
             if s == 6:
                 quant_r(1)
             if s < 7:
-                leaky(s, nc.gpsimd, 0, 2 * QW)
+                leaky(s, nc.gpsimd, 0, POOL_COLS)
+            if s >= 3:
+                turn_f(s - 1)
             for job in turns[s]:
                 if job[0] == "c":
                     turn_c(job[1])
                 else:
                     turn_r(job[1], job[2])
-            if s >= 1:
+            if 1 <= s < 3:
                 turn_f(s - 1)
             empty_all()
             for job in widens[s]:
@@ -467,6 +478,7 @@ def tile_leaky_slope_reconstructor_d6_kernel(
         react(6)
         react(7)
         add_v(2)
+        leaky_rest(0, 4)
         reorder_r(7)
         quant_r(5)
         quant_r(4)
@@ -486,6 +498,7 @@ def tile_leaky_slope_reconstructor_d6_kernel(
         react(11)
         add_v(6)
         add_v(7)
+        leaky_rest(4, 7)
         quant_r(7)
         weigh(9)
         quant_r(6)

@@ -30,7 +30,7 @@ NPAIR = NT // 2
 NH = 2 * NQ
 HEAD_C = 4
 C_LOADS = ((0, 1), (1, 5), (5, 8))
-PLAIN = (0, 2, 4, 6)
+RUNS = (2, 3)
 NGAINED = 8
 REVERSE_FROM = 3
 POOL_COLS = 448
@@ -172,22 +172,35 @@ def tile_leaky_slope_reconstructor_d6_kernel(
             first = (SPAN // P) * (h % 2)
             return r_sc[:, h // 2, first : first + SPAN // P]
 
-        def widen_r(h, r):
-            row = slice(SPAN * r, SPAN * (r + 1))
-            room = wide_r(h) if h in PLAIN else r_plain[(h // 2) % 2]
-            widen_row(room[:, row], raw_r(h)[:, row], r_scales(h), False)
+        def blocks_of(h, r, passes):
+            for g in passes:
+                for j in range(4 * g, 4 * g + 4):
+                    yield_raw = raw_r(h)[:, SPAN * r + P * j : SPAN * r + P * (j + 1)].bitcast(FP8)
+                    jobs.append((g, j, yield_raw, r_scales(h)[:, j : j + 1]))
 
-        def reorder_r(h, rows=slice(0, 2)):
-            src = r_plain[(h // 2) % 2][:].bitcast(F32).rearrange("p (r x u j) -> p u r x j", r=2, u=2, j=8)
-            dst = wide_r(h)[:].bitcast(F32).rearrange("p (u r x j) -> p u r x j", r=2, u=2, j=8)
-            nc.vector.tensor_copy(out=dst[:, :, rows], in_=src[:, :, rows])
+        jobs = []
 
-        def widen_r_ordered(h, r):
-            dst = wide_r(h)[:].rearrange("p (u r j b i) -> p r j b u i", u=2, r=2, b=4, i=16)
-            src = raw_r(h).rearrange("p (r j b u i) -> p r j b u i", r=2, b=4, u=2, i=16)
-            for j in range(SPAN // P):
+        def widen_r(h, r, passes=(0, 1)):
+            jobs.clear()
+            blocks_of(h, r, passes)
+            for g, j, raw, scale in jobs:
+                room = r_plain[(h // 2) % 2] if 2 * (h % 2) + g in RUNS else wide_r(h)
+                first = SPAN * g + 512 * r + P * (j % 4)
+                nc.scalar.activation(out=room[:, first : first + P], in_=raw, func=COPY, scale=scale)
+
+        def reorder_r(h, passes=slice(0, 2), on_vector=True):
+            src = r_plain[(h // 2) % 2][:].bitcast(F32).rearrange("p (g x u j) -> p g u x j", g=2, u=2, j=8)
+            dst = wide_r(h)[:].bitcast(F32).rearrange("p (g u x j) -> p g u x j", g=2, u=2, j=8)
+            copy = nc.vector.tensor_copy if on_vector else nc.scalar.copy
+            copy(out=dst[:, passes], in_=src[:, passes])
+
+        def widen_r_ordered(h, r, passes=(0, 1)):
+            jobs.clear()
+            blocks_of(h, r, passes)
+            dst = wide_r(h)[:].rearrange("p (g u r q b i) -> p g r q b u i", g=2, u=2, r=2, b=4, i=16)
+            for g, j, raw, scale in jobs:
                 nc.vector.tensor_scalar(
-                    out=dst[:, r, j], in0=src[:, r, j].bitcast(FP8), scalar1=r_scales(h)[:, j : j + 1], scalar2=None, op0=MULT
+                    out=dst[:, g, r, j % 4], in0=raw.rearrange("p (b u i) -> p b u i", u=2, i=16), scalar1=scale, scalar2=None, op0=MULT
                 )
 
         def c_four(i):
@@ -232,11 +245,11 @@ def tile_leaky_slope_reconstructor_d6_kernel(
             bank = next_bank()
             for r in range(2):
                 for u in range(2):
-                    if h in PLAIN:
-                        w0 = 512 * r + 256 * g + u
+                    if 2 * (h % 2) + g not in RUNS:
+                        w0 = 512 * g + 256 * r + u
                         nc.tensor.transpose(bank[:, r, u, :], words[:, w0 : w0 + 255 : 2], ident[:])
                     else:
-                        w0 = P * (4 * u + 2 * r + g)
+                        w0 = P * (4 * g + 2 * u + r)
                         nc.tensor.transpose(bank[:, r, u, :], words[:, w0 : w0 + P], ident[:])
             filled.append((bank, r_four(h)[:, g].bitcast(F32).rearrange("p (a r) u -> p a r u", r=2), bank[:].rearrange("p r u a -> p a r u")))
 
@@ -271,7 +284,7 @@ def tile_leaky_slope_reconstructor_d6_kernel(
                     add_slopes(i, n - 1)
 
         def add_slopes(i, n):
-            run = 2 if n < 2 else 16
+            run = 16 if n in RUNS else 2
             nc.vector.tensor_tensor(
                 out=full[(2 * i + n // 2) % 4][:, n % 2].rearrange("p u w e -> p u (w e)").rearrange("p u (w e) -> p u w e", e=run),
                 in0=acc[n][:].rearrange("p (w u e) -> p u w e", u=2, e=run),
@@ -401,8 +414,6 @@ def tile_leaky_slope_reconstructor_d6_kernel(
 
         for s in range(NT):
             mirror(s)
-            if s == 1:
-                leaky(7, nc.vector, 0, 2 * QW)
             if s == 2:
                 quant_r(0)
             if s == 4:
@@ -415,6 +426,8 @@ def tile_leaky_slope_reconstructor_d6_kernel(
                 quant_r(1)
             if s < 7:
                 leaky(s, nc.gpsimd, 0, POOL_COLS)
+            if s == 1:
+                leaky(7, nc.vector, 0, 2 * QW)
             if s >= 3:
                 turn_f(s - 1)
             for job in turns[s]:
@@ -452,11 +465,13 @@ def tile_leaky_slope_reconstructor_d6_kernel(
         widen_r(4, 1)
         widen_r(7, 0)
         widen_r(7, 1)
+        wide_r(5)
+        wide_r(6)
         react(1)
         react(2)
+        widen_r_ordered(5, 0)
         quant_f(6)
         quant_r(2)
-        widen_r_ordered(5, 0)
         widen_r_ordered(5, 1)
         quant_f(7)
         add_g(0, spare(f_ring[1][:].rearrange("p s a -> p (s a)")))
@@ -472,6 +487,7 @@ def tile_leaky_slope_reconstructor_d6_kernel(
         weigh(4)
         both(5)
         both(4)
+        reorder_r(7, slice(0, 2), False)
         widen_r(6, 0)
         widen_r(6, 1)
         react(5)
@@ -479,7 +495,7 @@ def tile_leaky_slope_reconstructor_d6_kernel(
         react(7)
         add_v(2)
         leaky_rest(0, 4)
-        reorder_r(7)
+        leaky_rest(4, 7)
         quant_r(5)
         quant_r(4)
         add_g(4, spare(s_sb[4]))
@@ -498,12 +514,12 @@ def tile_leaky_slope_reconstructor_d6_kernel(
         react(11)
         add_v(6)
         add_v(7)
-        leaky_rest(4, 7)
+        add_v(8)
         quant_r(7)
         weigh(9)
+        add_g(9, left_of(9))
+        store()
         quant_r(6)
-        add_g(9, spare(s_sb[6]))
-        add_v(8)
         react(12)
         react(13)
         weigh(10)

@@ -56,7 +56,8 @@ def tile_leaky_slope_reconstructor_d6_kernel(
         g_sc = tiles("g_sc", 1, [P, GA, L], U8)[0]
         r_raw = tiles("r_raw", NH, [P, L], U8)
         r_sc = tiles("r_sc", 1, [P, NQ, L // P], F32)[0]
-        s_sb = tiles("s_sb", NT, [P, L], BF16)
+        s_all = tiles("s_all", 1, [P, NT * L], BF16)[0]
+        s_sb = [s_all[:, L * i : L * (i + 1)] for i in range(NT)]
         prev_all = tiles("prev_all", 1, [P, NT * A], BF16)[0][:].rearrange("p (k s a) -> p k s a", k=NT, s=2)
         prev_sb = [prev_all[:, k] for k in range(NT)]
         gain_sb = tiles("gain_sb", 1, [P, A], BF16)[0]
@@ -68,16 +69,17 @@ def tile_leaky_slope_reconstructor_d6_kernel(
         r_plain = tiles("r_plain", 2, [P, 2 * SPAN], BF16)
         c_codes = tiles("c_codes", 3, [P, GA * P], U32)
         c_planes = tiles("c_planes", 3, [P, GA * P], U8)
-        r_codes = tiles("r_codes", 2 * NQ, [P, 2 * QW], U32)
-        r_planes = tiles("r_planes", 2 * NQ, [P, 2 * QW], U8)
+        r_codes = tiles("r_codes", NQ, [P, GL * QW], U32)
+        r_planes = tiles("r_planes", NQ, [P, GL * QW], U8)
         full = tiles("full", 4, [P, 2, 2, P, 2], BF16)
         f_ring = tiles("f_ring", 2, [P, 2, 2 * QW], F32)
         f_codes = tiles("f_codes", NT, [P, GL * P], U32)
         f_planes = tiles("f_planes", NT, [P, GL * P], U8)
         left_all = tiles("left_all", 1, [P, NT * A], F32)[0][:].rearrange("p (k s a) -> p k s a", k=NT, s=2)
         left = [left_all[:, k] for k in range(NT)]
-        c_ring = tiles("c_ring", 3, [P, 2 * QW], F32)
-        gained = tiles("gained", NGAINED, [P, 2, QW], F32)
+        c_ring = tiles("c_ring", 4, [P, 2 * QW], F32)
+        gained_all = tiles("gained_all", 1, [P, NGAINED * 2 * QW], F32)[0][:].rearrange("p (k s a) -> p k s a", s=2, a=QW)
+        gained = [gained_all[:, k] for k in range(NGAINED)]
         acc = [psum.tile([P, 512], F32, name="acc%d" % k) for k in range(4)]
         turn_bank = [psum.tile([P, 2, 2, P], F32, name="turn%d" % k) for k in range(4)]
 
@@ -204,7 +206,7 @@ def tile_leaky_slope_reconstructor_d6_kernel(
                 )
 
         def c_four(i):
-            room = left[i - 2][:, 0, :] if i in (2, 3) else c_ring[i % len(c_ring)][:]
+            room = left[i - 2][:, 0, :] if i in (2, 3) else c_ring[i % len(c_ring) if i != 4 else 2][:]
             return room.bitcast(BF16).rearrange("p (g r j) -> p g r j", g=GA, j=4)
 
         def f_four(i):
@@ -260,7 +262,11 @@ def tile_leaky_slope_reconstructor_d6_kernel(
             quantize(c_codes[i % 3], c_planes[i % 3], c_four(i))
 
         def quant_r(h):
-            quantize(r_codes[h], r_planes[h], r_four(h))
+            cols = slice(2 * QW * (h % 2), 2 * QW * (h % 2 + 1))
+            quantize(r_codes[h // 2][:, cols], r_planes[h // 2][:, cols], r_four(h))
+
+        def quant_q(q):
+            nc.vector.quantize_mx(out=r_codes[q][:].bitcast(FP8X4), scales=r_planes[q][:], in_=s_all[:, 2 * L * q : 2 * L * (q + 1)])
 
         def quant_f(i):
             quantize(f_codes[i], f_planes[i], f_four(i))
@@ -310,10 +316,12 @@ def tile_leaky_slope_reconstructor_d6_kernel(
             rates = leak_sb[:, base + first : base + end].unsqueeze(1).to_broadcast([P, 2, end - first])
             engine.tensor_tensor(out=left[k][:, :, first:end], in0=prev_sb[k][:, :, first:end], in1=rates, op=MULT)
 
-        def leaky_rest(first, end):
-            base = 2 * QW * (first // NPAIR)
-            rates = leak_sb[:, base + POOL_COLS : base + 2 * QW].unsqueeze(1).unsqueeze(1).to_broadcast([P, end - first, 2, 2 * QW - POOL_COLS])
-            nc.vector.tensor_tensor(out=left_all[:, first:end, :, POOL_COLS:], in0=prev_all[:, first:end, :, POOL_COLS:], in1=rates, op=MULT)
+        def leaky_rest():
+            rates = leak_sb[:].rearrange("p (h a) -> p h a", h=2)[:, :, POOL_COLS:].unsqueeze(2).to_broadcast([P, 2, NT, 2 * QW - POOL_COLS])
+            view = "p (h m) s a -> p h (m s) a"
+            nc.vector.tensor_tensor(
+                out=left_all.rearrange(view, h=2)[:, :, :, POOL_COLS:], in0=prev_all.rearrange(view, h=2)[:, :, :, POOL_COLS:], in1=rates, op=MULT
+            )
 
         def left_of(unit):
             q, m = unit // NPAIR, unit % NPAIR
@@ -324,15 +332,15 @@ def tile_leaky_slope_reconstructor_d6_kernel(
             bank = acc[(unit + shift) % 4]
             for side in range(sides.start, sides.stop):
                 i = 2 * m + side
-                passes = (0, 1, 2, 3) if q < 2 else (2, 3, 0, 1)
+                passes = (0, 1, 2, 3) if q < 1 else (2, 3, 0, 1)
                 for g in passes:
-                    cols = slice(QW * (g % 2), QW * (g % 2 + 1))
+                    cols = slice(QW * g, QW * (g + 1))
                     nc.tensor.matmul_mx(
                         out=bank[:, QW * side : QW * (side + 1)],
                         lhsT=f_codes[i][:, P * g : P * (g + 1)].bitcast(FP8X4),
                         lhsT_scale=f_planes[i][:, P * g : P * (g + 1)],
-                        rhs=r_codes[2 * q + g // 2][:, cols].bitcast(FP8X4),
-                        rhs_scale=r_planes[2 * q + g // 2][:, cols],
+                        rhs=r_codes[q][:, cols].bitcast(FP8X4),
+                        rhs_scale=r_planes[q][:, cols],
                         start=(g == passes[0]),
                         stop=(g == passes[-1]),
                     )
@@ -382,23 +390,30 @@ def tile_leaky_slope_reconstructor_d6_kernel(
         warm_up(4)
         widen_c(0, True)
         wide_c(2)
+        wide_c(4)
         turn_c(0)
         empty_all()
         widen_c(4, False, range(0, 2))
         widen_c(1, True)
+        warm_up(1)
+        turn_c(1)
+        empty_all()
+        widen_c(4, False, range(2, 4))
         widen_c(2, True)
         quant_c(0)
         widen_c(3, True)
-        for i in range(1, HEAD_C - 1):
-            warm_up(1)
-            turn_c(i)
-            empty_all()
-            widen_c(4, False, range(2 * i, 4 * i))
+        widen_c(4, True, range(4, 8))
+        warm_up(1)
+        turn_c(2)
+        empty_all()
         spread(r_col[:], acc[1])
         spread(leak_col[:].bitcast(F32), acc[2])
-        turn_c(HEAD_C - 1)
-        empty_all()
         warm_up(1)
+        turn_c(3)
+        empty_all()
+        turn_c(4)
+        empty_all()
+        warm_up(0)
         for side in range(2):
             part = slice(64 * side, 64 * (side + 1))
             nc.vector.tensor_copy(
@@ -407,7 +422,7 @@ def tile_leaky_slope_reconstructor_d6_kernel(
         quant_c(1)
         gather(acc[2], leak_sb[:].bitcast(F32))
 
-        turns = [[("c", 4)], [("r", 0, 0), ("r", 0, 1)], [("c", 5)], [("c", 6)], [("c", 7)], [("r", 1, 0), ("r", 1, 1)], [("r", 2, 0)], [("r", 2, 1)]]
+        turns = [[], [("r", 0, 0), ("r", 0, 1)], [("c", 5)], [("c", 6)], [("c", 7)], [("r", 1, 0), ("r", 1, 1)], [("r", 2, 0)], [("r", 2, 1)]]
         widens = [[("c", 5), ("c", 6)], [("c", 7)], [("r", 1, 0), ("r", 1, 1)], [("r", 2, 0)], [("r", 2, 1), ("r", 3, 0)], [("r", 3, 1)], [("r", 4, 0)], []]
         widen_r(0, 0)
         widen_r(0, 1)
@@ -427,7 +442,7 @@ def tile_leaky_slope_reconstructor_d6_kernel(
             if s < 7:
                 leaky(s, nc.gpsimd, 0, POOL_COLS)
             if s == 1:
-                leaky(7, nc.vector, 0, 2 * QW)
+                leaky(7, nc.vector, 0, POOL_COLS)
             if s >= 3:
                 turn_f(s - 1)
             for job in turns[s]:
@@ -452,6 +467,14 @@ def tile_leaky_slope_reconstructor_d6_kernel(
         def add_v(unit):
             finish(unit, nc.vector, left_of(unit))
 
+        def add_two(unit):
+            q, m = unit // NPAIR, unit % NPAIR
+            first = NPAIR * (q // 2) + m
+            both_left = left_all[:, first : first + 2, :, QW * (q % 2) : QW * (q % 2 + 1)].rearrange("p k s a -> p (k s) a")
+            both_gained = gained_all[:, unit % NGAINED : unit % NGAINED + 2].rearrange("p k s a -> p (k s) a")
+            nc.vector.tensor_tensor(out=both_left, in0=both_gained, in1=both_left, op=ADD)
+            nc.sync.dma_start(out=o_v[:, 2 * m : 2 * m + 4, QW * q : QW * (q + 1)], in_=both_left)
+
         def add_g(unit, room):
             finish(unit, nc.gpsimd, room)
 
@@ -471,12 +494,12 @@ def tile_leaky_slope_reconstructor_d6_kernel(
         react(2)
         widen_r_ordered(5, 0)
         quant_f(6)
-        quant_r(2)
         widen_r_ordered(5, 1)
         quant_f(7)
-        add_g(0, spare(f_ring[1][:].rearrange("p s a -> p (s a)")))
-        store()
         quant_r(3)
+        add_g(0, spare(s_sb[3]))
+        store()
+        quant_r(2)
         react(3)
         react(4)
         weigh(1)
@@ -494,8 +517,7 @@ def tile_leaky_slope_reconstructor_d6_kernel(
         react(6)
         react(7)
         add_v(2)
-        leaky_rest(0, 4)
-        leaky_rest(4, 7)
+        leaky_rest()
         quant_r(5)
         quant_r(4)
         add_g(4, spare(s_sb[4]))
@@ -512,8 +534,7 @@ def tile_leaky_slope_reconstructor_d6_kernel(
         react(9)
         react(10)
         react(11)
-        add_v(6)
-        add_v(7)
+        add_two(6)
         add_v(8)
         quant_r(7)
         weigh(9)
@@ -536,7 +557,8 @@ def tile_leaky_slope_reconstructor_d6_kernel(
         add_v(12)
         weigh(14)
         weigh(last, slice(0, 1))
-        weigh(last, slice(1, 2), 1)
+        store()
         add_v(14)
+        weigh(last, slice(1, 2), 1)
         finish(last, nc.vector, left_of(last), slice(0, 1))
         finish(last, nc.vector, left_of(last), slice(1, 2))

@@ -29,7 +29,7 @@ NQ = A // QW
 NPAIR = NT // 2
 NH = 2 * NQ
 HEAD_C = 4
-C_LOADS = ((0, 1), (1, 5), (5, 8))
+C_LOADS = ((0, 1), (1, 5), (5, 6), (6, 8))
 RUNS = (2, 3)
 NGAINED = 8
 REVERSE_FROM = 3
@@ -114,8 +114,11 @@ def tile_leaky_slope_reconstructor_d6_kernel(
             half, m = k // NPAIR, k % NPAIR
             nc.sync.dma_start(out=prev_sb[k][:], in_=p_v[:, 2 * m : 2 * m + 2, 2 * QW * half : 2 * QW * (half + 1)])
 
-        nc.vector.memset(g_sc[:].rearrange("p g n -> p (g n)").bitcast(I32), 0)
-        make_identity(nc, ident[:])
+        nc.vector.memset(ident[:], 0.0)
+        make_identity(nc, ident[:], nomemset=True)
+        g_fill = g_sc[:].rearrange("p g n -> p (g n)").bitcast(I32)
+        nc.vector.memset(g_fill[:, 0:513], 0)
+        nc.vector.memset(g_fill[:, 513:1024], 0)
         nc.sync.dma_start(out=c_sc[:], in_=C_scale.rearrange("(p i) j -> p i j", i=NT))
         load_c(0)
         nc.sync.dma_start(out=r_col[:], in_=R_scale.rearrange("i (j o) -> (i j) o", o=1))
@@ -128,12 +131,13 @@ def tile_leaky_slope_reconstructor_d6_kernel(
                 in_=G_scales[:, r:16:4, :].rearrange("g q n -> q g n").bitcast(I32),
             )
         load_g(1)
+        load_c(2)
         load_s_half(0, 0)
         load_r(0)
         load_s_half(0, 1)
         load_s(1)
         load_prev(0)
-        load_c(2)
+        load_c(3)
         load_prev(7)
         load_prev(1)
         load_s(2)
@@ -423,7 +427,8 @@ def tile_leaky_slope_reconstructor_d6_kernel(
         gather(acc[2], leak_sb[:].bitcast(F32))
 
         turns = [[], [("r", 0, 0), ("r", 0, 1)], [("c", 5)], [("c", 6)], [("c", 7)], [("r", 1, 0), ("r", 1, 1)], [("r", 2, 0)], [("r", 2, 1)]]
-        widens = [[("c", 5), ("c", 6)], [("c", 7)], [("r", 1, 0), ("r", 1, 1)], [("r", 2, 0)], [("r", 2, 1), ("r", 3, 0)], [("r", 3, 1)], [("r", 4, 0)], []]
+        widens = [[("c", 6)], [("c", 7)], [("r", 1, 0), ("r", 1, 1)], [("r", 2, 0)], [("r", 2, 1), ("r", 3, 0)], [("r", 3, 1)], [("r", 4, 0)], []]
+        widen_c(5, False)
         widen_r(0, 0)
         widen_r(0, 1)
 
@@ -467,13 +472,14 @@ def tile_leaky_slope_reconstructor_d6_kernel(
         def add_v(unit):
             finish(unit, nc.vector, left_of(unit))
 
-        def add_two(unit):
+        def add_sides(unit, first, end):
             q, m = unit // NPAIR, unit % NPAIR
-            first = NPAIR * (q // 2) + m
-            both_left = left_all[:, first : first + 2, :, QW * (q % 2) : QW * (q % 2 + 1)].rearrange("p k s a -> p (k s) a")
-            both_gained = gained_all[:, unit % NGAINED : unit % NGAINED + 2].rearrange("p k s a -> p (k s) a")
-            nc.vector.tensor_tensor(out=both_left, in0=both_gained, in1=both_left, op=ADD)
-            nc.sync.dma_start(out=o_v[:, 2 * m : 2 * m + 4, QW * q : QW * (q + 1)], in_=both_left)
+            count = (end + 1) // 2
+            at = NPAIR * (q // 2) + m
+            old = left_all[:, at : at + count, :, QW * (q % 2) : QW * (q % 2 + 1)].rearrange("p k s a -> p (k s) a")[:, first:end]
+            new = gained_all[:, unit % NGAINED : unit % NGAINED + count].rearrange("p k s a -> p (k s) a")[:, first:end]
+            nc.vector.tensor_tensor(out=old, in0=new, in1=old, op=ADD)
+            nc.sync.dma_start(out=o_v[:, 2 * m + first : 2 * m + end, QW * q : QW * (q + 1)], in_=old)
 
         def add_g(unit, room):
             finish(unit, nc.gpsimd, room)
@@ -503,7 +509,7 @@ def tile_leaky_slope_reconstructor_d6_kernel(
         react(3)
         react(4)
         weigh(1)
-        add_g(1, left_of(1))
+        finish(1, nc.gpsimd, left_of(1), slice(0, 1))
         store()
         weigh(2)
         weigh(3)
@@ -516,7 +522,7 @@ def tile_leaky_slope_reconstructor_d6_kernel(
         react(5)
         react(6)
         react(7)
-        add_v(2)
+        add_sides(1, 1, 4)
         leaky_rest()
         quant_r(5)
         quant_r(4)
@@ -524,7 +530,7 @@ def tile_leaky_slope_reconstructor_d6_kernel(
         add_v(3)
         react(8)
         weigh(5)
-        add_g(5, left_of(5))
+        finish(5, nc.gpsimd, left_of(5), slice(0, 1))
         store()
         weigh(6)
         weigh(7)
@@ -534,7 +540,7 @@ def tile_leaky_slope_reconstructor_d6_kernel(
         react(9)
         react(10)
         react(11)
-        add_two(6)
+        add_sides(5, 1, 6)
         add_v(8)
         quant_r(7)
         weigh(9)
@@ -557,8 +563,8 @@ def tile_leaky_slope_reconstructor_d6_kernel(
         add_v(12)
         weigh(14)
         weigh(last, slice(0, 1))
+        weigh(last, slice(1, 2), 1)
         store()
         add_v(14)
-        weigh(last, slice(1, 2), 1)
         finish(last, nc.vector, left_of(last), slice(0, 1))
         finish(last, nc.vector, left_of(last), slice(1, 2))

@@ -32,8 +32,9 @@ HEAD_C = 4
 C_LOADS = ((0, 1), (1, 5), (5, 6), (6, 8))
 RUNS = (2, 3)
 NGAINED = 8
-REVERSE_FROM = 3
+REVERSE_FROM = 1
 POOL_COLS = 448
+UNIT_BANK = (0, 1, 2, 3, 0, 0, 3, 2, 1, 1, 2, 3, 0, 1, 2, 3, 0)
 SHARED_F = NT - 3
 SHARED_C = 3
 
@@ -225,6 +226,11 @@ def tile_leaky_slope_reconstructor_d6_kernel(
             free_banks.remove(bank)
             return bank
 
+        def newest_first(count):
+            order = list(reversed(free_banks[:count])) + free_banks[count:]
+            free_banks.clear()
+            free_banks.extend(order)
+
         def empty_all():
             for bank, dst, src in reversed(filled):
                 nc.scalar.copy(out=dst, in_=src)
@@ -249,7 +255,7 @@ def tile_leaky_slope_reconstructor_d6_kernel(
         def turn_r(h, g):
             words = wide_r(h)[:].bitcast(F32)
             bank = next_bank()
-            for r in range(2):
+            for r in (1, 0):
                 for u in range(2):
                     if 2 * (h % 2) + g not in RUNS:
                         w0 = 512 * g + 256 * r + u
@@ -333,7 +339,7 @@ def tile_leaky_slope_reconstructor_d6_kernel(
 
         def react(unit, sides=slice(0, 2), shift=0):
             q, m = unit // NPAIR, unit % NPAIR
-            bank = acc[(unit + shift) % 4]
+            bank = acc[UNIT_BANK[unit + shift]]
             for side in range(sides.start, sides.stop):
                 i = 2 * m + side
                 passes = (0, 1, 2, 3) if q < 1 else (2, 3, 0, 1)
@@ -351,7 +357,7 @@ def tile_leaky_slope_reconstructor_d6_kernel(
 
         def weigh(unit, sides=slice(0, 2), shift=0):
             q = unit // NPAIR
-            bank = acc[(unit + shift) % 4]
+            bank = acc[UNIT_BANK[unit + shift]]
             nc.vector.tensor_tensor(
                 out=gained[unit % NGAINED][:, sides, :],
                 in0=bank[:].rearrange("p (s a) -> p s a", s=2)[:, sides, :],
@@ -426,7 +432,7 @@ def tile_leaky_slope_reconstructor_d6_kernel(
         quant_c(1)
         gather(acc[2], leak_sb[:].bitcast(F32))
 
-        turns = [[], [("r", 0, 0), ("r", 0, 1)], [("c", 5)], [("c", 6)], [("c", 7)], [("r", 1, 0), ("r", 1, 1)], [("r", 2, 0)], [("r", 2, 1)]]
+        turns = [[], [("r", 0, 1), ("r", 0, 0)], [("c", 5)], [("c", 6)], [("c", 7)], [("r", 1, 0), ("r", 1, 1)], [("r", 2, 0)], [("r", 2, 1)]]
         widens = [[("c", 6)], [("c", 7)], [("r", 1, 0), ("r", 1, 1)], [("r", 2, 0)], [("r", 2, 1), ("r", 3, 0)], [("r", 3, 1)], [("r", 4, 0)], []]
         widen_c(5, False)
         widen_r(0, 0)
@@ -448,6 +454,7 @@ def tile_leaky_slope_reconstructor_d6_kernel(
                 leaky(s, nc.gpsimd, 0, POOL_COLS)
             if s == 1:
                 leaky(7, nc.vector, 0, POOL_COLS)
+            newest_first(2 + len(turns[s]))
             if s >= 3:
                 turn_f(s - 1)
             for job in turns[s]:
@@ -465,8 +472,8 @@ def tile_leaky_slope_reconstructor_d6_kernel(
                     widen_r(job[1], job[2])
 
         def both(h):
-            turn_r(h, 0)
             turn_r(h, 1)
+            turn_r(h, 0)
             empty_all()
 
         def add_v(unit):

from contextlib import ExitStack

import concourse.mybir as mybir
from concourse.masks import make_identity

T, A, L = 1024, 1024, 2048
P = 128
FLOPS = 2 * T * A * L * 2

F32 = mybir.dt.float32
BF16 = mybir.dt.bfloat16
I32 = mybir.dt.int32
U32 = mybir.dt.uint32
U8 = mybir.dt.uint8
FP8 = mybir.dt.float8_e4m3fn
FP8X4 = mybir.dt.float8_e4m3fn_x4
FP4X4 = mybir.dt.float4_e2m1fn_x4
MULT = mybir.AluOpType.mult
ADD = mybir.AluOpType.add
COPY = mybir.ActivationFunctionType.Copy

NT = T // P
GA = A // 512
GL = L // 512
NL = L // 512
SPAN = 1024
QW = 256
NQ = A // QW
NPAIR = NT // 2
NH = 2 * NQ
HEAD_C = 4
C_LOADS = ((0, 1), (1, 5), (5, 6), (6, 8))
RUNS = (2, 3)
NGAINED = 8
REVERSE_FROM = 1
POOL_COLS = 448
UNIT_BANK = (0, 1, 2, 3, 0, 0, 3, 2, 1, 1, 2, 3, 0, 1, 2, 3, 0)
SHARED_F = NT - 3
SHARED_C = 3


def tile_leaky_slope_reconstructor_d6_kernel(
    tc, C_bytes, C_scale, G_words, G_scales, slopes, R_bytes, R_scale, gain, leak, prev, out
):
    nc = tc.nc
    with ExitStack() as ctx:
        keep = ctx.enter_context(tc.tile_pool(name="keep", bufs=1))
        psum = ctx.enter_context(tc.psum_pool(name="psum", bufs=1))
        ctx.enter_context(tc.manual_schedule())

        def tiles(name, count, shape, dtype):
            return [keep.tile(shape, dtype, align_bytes=64, name="%s%d" % (name, k)) for k in range(count)]

        c_raw = [tiles("c_raw%d_" % first, 1, [P, end - first, A], U8)[0] for first, end in C_LOADS]
        c_sc = tiles("c_sc", 1, [P, NT, A // P], F32)[0]
        g_words = tiles("g_words", NL // 2, [P, GA, L], U8)
        g_sc = tiles("g_sc", 1, [P, GA, L], U8)[0]
        r_raw = tiles("r_raw", NH, [P, L], U8)
        r_sc = tiles("r_sc", 1, [P, NQ, L // P], F32)[0]
        s_all = tiles("s_all", 1, [P, NT * L], BF16)[0]
        s_sb = [s_all[:, L * i : L * (i + 1)] for i in range(NT)]
        prev_all = tiles("prev_all", 1, [P, NT * A], BF16)[0][:].rearrange("p (k s a) -> p k s a", k=NT, s=2)
        prev_sb = [prev_all[:, k] for k in range(NT)]
        gain_sb = tiles("gain_sb", 1, [P, A], BF16)[0]
        leak_sb = tiles("leak_sb", 1, [P, A], BF16)[0]
        r_col = tiles("r_col", 1, [P, 1], F32)[0]
        leak_col = tiles("leak_col", 1, [P, A // P], BF16)[0]
        ident = tiles("ident", 1, [P, P], F32)[0]
        wide = tiles("wide", 4, [P, 2 * SPAN], BF16)
        r_plain = tiles("r_plain", 2, [P, 2 * SPAN], BF16)
        c_codes = tiles("c_codes", 3, [P, GA * P], U32)
        c_planes = tiles("c_planes", 3, [P, GA * P], U8)
        r_codes = tiles("r_codes", NQ, [P, GL * QW], U32)
        r_planes = tiles("r_planes", NQ, [P, GL * QW], U8)
        full = tiles("full", 4, [P, 2, 2, P, 2], BF16)
        f_ring = tiles("f_ring", 2, [P, 2, 2 * QW], F32)
        f_codes = tiles("f_codes", NT, [P, GL * P], U32)
        f_planes = tiles("f_planes", NT, [P, GL * P], U8)
        left_all = tiles("left_all", 1, [P, NT * A], F32)[0][:].rearrange("p (k s a) -> p k s a", k=NT, s=2)
        left = [left_all[:, k] for k in range(NT)]
        c_ring = tiles("c_ring", 4, [P, 2 * QW], F32)
        gained_all = tiles("gained_all", 1, [P, NGAINED * 2 * QW], F32)[0][:].rearrange("p (k s a) -> p k s a", s=2, a=QW)
        gained = [gained_all[:, k] for k in range(NGAINED)]
        acc = [psum.tile([P, 512], F32, name="acc%d" % k) for k in range(4)]
        turn_bank = [psum.tile([P, 2, 2, P], F32, name="turn%d" % k) for k in range(4)]

        c_v = C_bytes.rearrange("(p i) k -> p i k", i=NT)
        s_v = slopes.rearrange("(p i) l -> p i l", i=NT)
        p_v = prev.rearrange("(p i) a -> p i a", i=NT)
        o_v = out.rearrange("(p i) a -> p i a", i=NT)
        r_v = R_bytes.rearrange("(q p r) l -> q p r l", p=P, r=2)
        g_v = G_words.rearrange("g p n -> p g n")

        def load_c(m):
            first, end = C_LOADS[m]
            nc.sync.dma_start(out=c_raw[m][:], in_=c_v[:, first:end, :])

        def load_g(n):
            nc.sync.dma_start(out=g_words[n][:].bitcast(I32), in_=g_v[:, :, L * n : L * (n + 1)].bitcast(I32))

        def load_s_half(i, h):
            nc.sync.dma_start(out=s_sb[i][:, SPAN * h : SPAN * (h + 1)], in_=s_v[:, i, SPAN * h : SPAN * (h + 1)])

        def load_s(i):
            nc.sync.dma_start(out=s_sb[i][:], in_=s_v[:, i, :])

        def raw_r(h):
            return r_raw[h][:]

        def load_r(h):
            rows = r_v[h // 2][:, :, SPAN * (h % 2) : SPAN * (h % 2 + 1)]
            nc.sync.dma_start(out=raw_r(h).rearrange("p (r k) -> p r k", r=2), in_=rows)

        def load_prev(k):
            half, m = k // NPAIR, k % NPAIR
            nc.sync.dma_start(out=prev_sb[k][:], in_=p_v[:, 2 * m : 2 * m + 2, 2 * QW * half : 2 * QW * (half + 1)])

        nc.vector.memset(ident[:], 0.0)
        make_identity(nc, ident[:], nomemset=True)
        g_fill = g_sc[:].rearrange("p g n -> p (g n)").bitcast(I32)
        nc.vector.memset(g_fill[:, 0:513], 0)
        nc.vector.memset(g_fill[:, 513:1024], 0)
        nc.sync.dma_start(out=c_sc[:], in_=C_scale.rearrange("(p i) j -> p i j", i=NT))
        load_c(0)
        nc.sync.dma_start(out=r_col[:], in_=R_scale.rearrange("i (j o) -> (i j) o", o=1))
        nc.sync.dma_start(out=leak_col[:], in_=leak.rearrange("(p e) -> p e", p=P))
        load_c(1)
        load_g(0)
        for r in range(4):
            nc.scalar.dma_start(
                out=g_sc[r:P:32, :, :].bitcast(I32),
                in_=G_scales[:, r:16:4, :].rearrange("g q n -> q g n").bitcast(I32),
            )
        load_g(1)
        load_c(2)
        load_s_half(0, 0)
        load_r(0)
        load_s_half(0, 1)
        load_s(1)
        load_prev(0)
        load_c(3)
        load_prev(7)
        load_prev(1)
        load_s(2)
        load_r(1)
        for s in range(3, NT):
            load_prev(s - 1)
            load_s(s)
            load_r(s - 1)
        load_r(7)
        nc.sync.dma_start(out=gain_sb[:], in_=gain.partition_broadcast(P))

        room_of = {}

        def wide_c(i):
            key = ("c", i // 2)
            room_of.setdefault(key, wide[len(room_of) % len(wide)])
            return room_of[key][:, A * (i % 2) : A * (i % 2 + 1)]

        def wide_r(h):
            room_of.setdefault(("r", h), wide[len(room_of) % len(wide)])
            return room_of[("r", h)]

        def widen_row(dst, raw, scale, on_vector, blocks=range(SPAN // P)):
            for j in blocks:
                k = slice(P * j, P * (j + 1))
                if on_vector:
                    nc.vector.tensor_scalar(
                        out=dst[:, k], in0=raw[:, k].bitcast(FP8), scalar1=scale[:, j : j + 1], scalar2=None, op0=MULT
                    )
                else:
                    nc.scalar.activation(out=dst[:, k], in_=raw[:, k].bitcast(FP8), func=COPY, scale=scale[:, j : j + 1])

        def widen_c(i, on_vector, blocks=range(SPAN // P)):
            m = sum(1 for first, end in C_LOADS if end <= i)
            widen_row(wide_c(i), c_raw[m][:, i - C_LOADS[m][0], :], c_sc[:, i, :], on_vector, blocks)

        def r_scales(h):
            first = (SPAN // P) * (h % 2)
            return r_sc[:, h // 2, first : first + SPAN // P]

        def blocks_of(h, r, passes):
            for g in passes:
                for j in range(4 * g, 4 * g + 4):
                    yield_raw = raw_r(h)[:, SPAN * r + P * j : SPAN * r + P * (j + 1)].bitcast(FP8)
                    jobs.append((g, j, yield_raw, r_scales(h)[:, j : j + 1]))

        jobs = []

        def widen_r(h, r, passes=(0, 1)):
            jobs.clear()
            blocks_of(h, r, passes)
            for g, j, raw, scale in jobs:
                room = r_plain[(h // 2) % 2] if 2 * (h % 2) + g in RUNS else wide_r(h)
                first = SPAN * g + 512 * r + P * (j % 4)
                nc.scalar.activation(out=room[:, first : first + P], in_=raw, func=COPY, scale=scale)

        def reorder_r(h, passes=slice(0, 2), on_vector=True):
            src = r_plain[(h // 2) % 2][:].bitcast(F32).rearrange("p (g x u j) -> p g u x j", g=2, u=2, j=8)
            dst = wide_r(h)[:].bitcast(F32).rearrange("p (g u x j) -> p g u x j", g=2, u=2, j=8)
            copy = nc.vector.tensor_copy if on_vector else nc.scalar.copy
            copy(out=dst[:, passes], in_=src[:, passes])

        def widen_r_ordered(h, r, passes=(0, 1)):
            jobs.clear()
            blocks_of(h, r, passes)
            dst = wide_r(h)[:].rearrange("p (g u r q b i) -> p g r q b u i", g=2, u=2, r=2, b=4, i=16)
            for g, j, raw, scale in jobs:
                nc.vector.tensor_scalar(
                    out=dst[:, g, r, j % 4], in0=raw.rearrange("p (b u i) -> p b u i", u=2, i=16), scalar1=scale, scalar2=None, op0=MULT
                )

        def c_four(i):
            room = left[i - 2][:, 0, :] if i in (2, 3) else c_ring[i % len(c_ring) if i != 4 else 2][:]
            return room.bitcast(BF16).rearrange("p (g r j) -> p g r j", g=GA, j=4)

        def f_four(i):
            room = left[i + 2] if i < SHARED_F else f_ring[i % 2]
            return room[:].rearrange("p s a -> p (s a)").bitcast(BF16).rearrange("p (g r j) -> p g r j", g=GL, j=4)

        free_banks = list(turn_bank)
        filled = []

        def next_bank():
            bank = free_banks[0]
            free_banks.remove(bank)
            return bank

        def newest_first(count):
            order = list(reversed(free_banks[:count])) + free_banks[count:]
            free_banks.clear()
            free_banks.extend(order)

        def empty_all():
            for bank, dst, src in reversed(filled):
                nc.scalar.copy(out=dst, in_=src)
                free_banks.append(bank)
            filled.clear()

        def turn_c(i):
            words = wide_c(i).bitcast(F32)
            bank = next_bank()
            for g in range(2):
                for u in range(2):
                    w0 = 256 * g + u
                    nc.tensor.transpose(bank[:, g, u, :], words[:, w0 : w0 + 255 : 2], ident[:])
            empty(bank, c_four(i))

        def empty(bank, dst):
            filled.append((bank, dst.bitcast(F32), bank[:].rearrange("p g u r -> p g r u")))

        def r_four(h):
            return s_sb[h][:].rearrange("p (g r j) -> p g r j", g=2, j=4)

        def turn_r(h, g):
            words = wide_r(h)[:].bitcast(F32)
            bank = next_bank()
            for r in (1, 0):
                for u in range(2):
                    if 2 * (h % 2) + g not in RUNS:
                        w0 = 512 * g + 256 * r + u
                        nc.tensor.transpose(bank[:, r, u, :], words[:, w0 : w0 + 255 : 2], ident[:])
                    else:
                        w0 = P * (4 * g + 2 * u + r)
                        nc.tensor.transpose(bank[:, r, u, :], words[:, w0 : w0 + P], ident[:])
            filled.append((bank, r_four(h)[:, g].bitcast(F32).rearrange("p (a r) u -> p a r u", r=2), bank[:].rearrange("p r u a -> p a r u")))

        def quantize(codes, planes, four):
            nc.vector.quantize_mx(out=codes[:].bitcast(FP8X4), scales=planes[:], in_=four.rearrange("p g r j -> p (g r j)"))

        def quant_c(i):
            quantize(c_codes[i % 3], c_planes[i % 3], c_four(i))

        def quant_r(h):
            cols = slice(2 * QW * (h % 2), 2 * QW * (h % 2 + 1))
            quantize(r_codes[h // 2][:, cols], r_planes[h // 2][:, cols], r_four(h))

        def quant_q(q):
            nc.vector.quantize_mx(out=r_codes[q][:].bitcast(FP8X4), scales=r_planes[q][:], in_=s_all[:, 2 * L * q : 2 * L * (q + 1)])

        def quant_f(i):
            quantize(f_codes[i], f_planes[i], f_four(i))

        def mirror(i):
            for n in range(NL):
                for g in range(GA):
                    nc.tensor.matmul_mx(
                        out=acc[n][:],
                        lhsT=c_codes[i % 3][:, P * g : P * (g + 1)].bitcast(FP8X4),
                        lhsT_scale=c_planes[i % 3][:, P * g : P * (g + 1)],
                        rhs=g_words[n // 2][:, g, 1024 * (n % 2) : 1024 * (n % 2 + 1)].bitcast(FP4X4),
                        rhs_scale=g_sc[:, g, 512 * n : 512 * (n + 1)],
                        start=(g == 0),
                        stop=(g == GA - 1),
                    )
                if i < REVERSE_FROM:
                    add_slopes(i, n)
                elif n % 2 == 1:
                    add_slopes(i, n)
                    add_slopes(i, n - 1)

        def add_slopes(i, n):
            run = 16 if n in RUNS else 2
            nc.vector.tensor_tensor(
                out=full[(2 * i + n // 2) % 4][:, n % 2].rearrange("p u w e -> p u (w e)").rearrange("p u (w e) -> p u w e", e=run),
                in0=acc[n][:].rearrange("p (w u e) -> p u w e", u=2, e=run),
                in1=s_sb[i][:, 512 * n : 512 * (n + 1)].rearrange("p (w u e) -> p u w e", u=2, e=run),
                op=ADD,
            )

        def turn_f(i):
            for h in range(2):
                words = full[(2 * i + h) % 4][:].rearrange("p g u w e -> p (g u w e)").bitcast(F32)
                bank = next_bank()
                for g in range(2):
                    for u in range(2):
                        w0 = P * (2 * g + u)
                        nc.tensor.transpose(bank[:, g, u, :], words[:, w0 : w0 + P], ident[:])
                empty(bank, f_four(i)[:, 2 * h : 2 * h + 2, :, :])

        def along(row, q):
            return row[:, QW * q : QW * (q + 1)].unsqueeze(1).to_broadcast([P, 2, QW])

        def leaky(k, engine, first, end):
            base = 2 * QW * (k // NPAIR)
            rates = leak_sb[:, base + first : base + end].unsqueeze(1).to_broadcast([P, 2, end - first])
            engine.tensor_tensor(out=left[k][:, :, first:end], in0=prev_sb[k][:, :, first:end], in1=rates, op=MULT)

        def leaky_rest():
            rates = leak_sb[:].rearrange("p (h a) -> p h a", h=2)[:, :, POOL_COLS:].unsqueeze(2).to_broadcast([P, 2, NT, 2 * QW - POOL_COLS])
            view = "p (h m) s a -> p h (m s) a"
            nc.vector.tensor_tensor(
                out=left_all.rearrange(view, h=2)[:, :, :, POOL_COLS:], in0=prev_all.rearrange(view, h=2)[:, :, :, POOL_COLS:], in1=rates, op=MULT
            )

        def left_of(unit):
            q, m = unit // NPAIR, unit % NPAIR
            return left[NPAIR * (q // 2) + m][:, :, QW * (q % 2) : QW * (q % 2 + 1)]

        def react(unit, sides=slice(0, 2), shift=0):
            q, m = unit // NPAIR, unit % NPAIR
            bank = acc[UNIT_BANK[unit + shift]]
            for side in range(sides.start, sides.stop):
                i = 2 * m + side
                passes = (0, 1, 2, 3) if q < 1 else (2, 3, 0, 1)
                for g in passes:
                    cols = slice(QW * g, QW * (g + 1))
                    nc.tensor.matmul_mx(
                        out=bank[:, QW * side : QW * (side + 1)],
                        lhsT=f_codes[i][:, P * g : P * (g + 1)].bitcast(FP8X4),
                        lhsT_scale=f_planes[i][:, P * g : P * (g + 1)],
                        rhs=r_codes[q][:, cols].bitcast(FP8X4),
                        rhs_scale=r_planes[q][:, cols],
                        start=(g == passes[0]),
                        stop=(g == passes[-1]),
                    )

        def weigh(unit, sides=slice(0, 2), shift=0):
            q = unit // NPAIR
            bank = acc[UNIT_BANK[unit + shift]]
            nc.vector.tensor_tensor(
                out=gained[unit % NGAINED][:, sides, :],
                in0=bank[:].rearrange("p (s a) -> p s a", s=2)[:, sides, :],
                in1=along(gain_sb, q)[:, sides, :],
                op=MULT,
            )

        stores = []

        def finish(unit, engine, result, sides=slice(0, 2)):
            q, m = unit // NPAIR, unit % NPAIR
            engine.tensor_tensor(out=result[:, sides, :], in0=gained[unit % NGAINED][:, sides, :], in1=left_of(unit)[:, sides, :], op=ADD)
            stores.append((o_v[:, 2 * m : 2 * m + 2, QW * q : QW * (q + 1)][:, sides, :], result[:, sides, :]))
            if engine is nc.vector:
                store()

        def store():
            for dst, src in reversed(stores):
                nc.sync.dma_start(out=dst, in_=src)
            stores.clear()

        def spread(words, bank):
            for j in range(words.shape[1]):
                nc.tensor.transpose(bank[:, P * j : P * (j + 1)], words[:, j : j + 1].to_broadcast([P, P]), ident[:])

        def gather(bank, dst):
            count = dst.shape[1] // P
            nc.vector.tensor_copy(
                out=dst.rearrange("p (n j) -> p n j", j=count),
                in_=bank[:, : P * count].rearrange("p (j n) -> p n j", j=count),
            )

        def warm_up(count):
            for k in range(count):
                nc.tensor.matmul(acc[3][:, 0:P], lhsT=ident[:], rhs=ident[:], start=True, stop=True)

        def spare(room):
            return room[:].bitcast(F32)[:, : 2 * QW].rearrange("p (s a) -> p s a", s=2)

        warm_up(4)
        widen_c(0, True)
        wide_c(2)
        wide_c(4)
        turn_c(0)
        empty_all()
        widen_c(4, False, range(0, 2))
        widen_c(1, True)
        warm_up(1)
        turn_c(1)
        empty_all()
        widen_c(4, False, range(2, 4))
        widen_c(2, True)
        quant_c(0)
        widen_c(3, True)
        widen_c(4, True, range(4, 8))
        warm_up(1)
        turn_c(2)
        empty_all()
        spread(r_col[:], acc[1])
        spread(leak_col[:].bitcast(F32), acc[2])
        warm_up(1)
        turn_c(3)
        empty_all()
        turn_c(4)
        empty_all()
        warm_up(0)
        for side in range(2):
            part = slice(64 * side, 64 * (side + 1))
            nc.vector.tensor_copy(
                out=r_sc[part], in_=acc[1][part, 0:P].rearrange("p (q s j) -> p q s j", s=2, j=L // P)[:, :, side, :]
            )
        quant_c(1)
        gather(acc[2], leak_sb[:].bitcast(F32))

        turns = [[], [("r", 0, 1), ("r", 0, 0)], [("c", 5)], [("c", 6)], [("c", 7)], [("r", 1, 0), ("r", 1, 1)], [("r", 2, 0)], [("r", 2, 1)]]
        widens = [[("c", 6)], [("c", 7)], [("r", 1, 0), ("r", 1, 1)], [("r", 2, 0)], [("r", 2, 1), ("r", 3, 0)], [("r", 3, 1)], [("r", 4, 0)], []]
        widen_c(5, False)
        widen_r(0, 0)
        widen_r(0, 1)

        for s in range(NT):
            mirror(s)
            if s == 2:
                quant_r(0)
            if s == 4:
                reorder_r(1)
            if 2 <= s < 7:
                quant_f(s - 2)
            if s + 2 < NT:
                quant_c(s + 2)
            if s == 6:
                quant_r(1)
            if s < 7:
                leaky(s, nc.gpsimd, 0, POOL_COLS)
            if s == 1:
                leaky(7, nc.vector, 0, POOL_COLS)
            newest_first(2 + len(turns[s]))
            if s >= 3:
                turn_f(s - 1)
            for job in turns[s]:
                if job[0] == "c":
                    turn_c(job[1])
                else:
                    turn_r(job[1], job[2])
            if 1 <= s < 3:
                turn_f(s - 1)
            empty_all()
            for job in widens[s]:
                if job[0] == "c":
                    widen_c(job[1], False)
                else:
                    widen_r(job[1], job[2])

        def both(h):
            turn_r(h, 1)
            turn_r(h, 0)
            empty_all()

        def add_v(unit):
            finish(unit, nc.vector, left_of(unit))

        def add_sides(unit, first, end):
            q, m = unit // NPAIR, unit % NPAIR
            count = (end + 1) // 2
            at = NPAIR * (q // 2) + m
            old = left_all[:, at : at + count, :, QW * (q % 2) : QW * (q % 2 + 1)].rearrange("p k s a -> p (k s) a")[:, first:end]
            new = gained_all[:, unit % NGAINED : unit % NGAINED + count].rearrange("p k s a -> p (k s) a")[:, first:end]
            nc.vector.tensor_tensor(out=old, in0=new, in1=old, op=ADD)
            nc.sync.dma_start(out=o_v[:, 2 * m + first : 2 * m + end, QW * q : QW * (q + 1)], in_=old)

        def add_g(unit, room):
            finish(unit, nc.gpsimd, room)

        react(0)
        reorder_r(3)
        quant_f(5)
        weigh(0)
        turn_f(NT - 1)
        empty_all()
        both(3)
        widen_r(4, 1)
        widen_r(7, 0)
        widen_r(7, 1)
        wide_r(5)
        wide_r(6)
        react(1)
        react(2)
        widen_r_ordered(5, 0)
        quant_f(6)
        widen_r_ordered(5, 1)
        quant_f(7)
        quant_r(3)
        add_g(0, spare(s_sb[3]))
        store()
        quant_r(2)
        react(3)
        react(4)
        weigh(1)
        finish(1, nc.gpsimd, left_of(1), slice(0, 1))
        store()
        weigh(2)
        weigh(3)
        weigh(4)
        both(5)
        both(4)
        reorder_r(7, slice(0, 2), False)
        widen_r(6, 0)
        widen_r(6, 1)
        react(5)
        react(6)
        react(7)
        add_sides(1, 1, 4)
        leaky_rest()
        quant_r(5)
        quant_r(4)
        add_g(4, spare(s_sb[4]))
        add_v(3)
        react(8)
        weigh(5)
        finish(5, nc.gpsimd, left_of(5), slice(0, 1))
        store()
        weigh(6)
        weigh(7)
        weigh(8)
        both(7)
        both(6)
        react(9)
        react(10)
        react(11)
        add_sides(5, 1, 6)
        add_v(8)
        quant_r(7)
        weigh(9)
        add_g(9, left_of(9))
        store()
        quant_r(6)
        react(12)
        react(13)
        weigh(10)
        weigh(11)
        react(14)
        add_g(11, left_of(11))
        add_v(10)
        last = 15
        react(last, slice(0, 1))
        weigh(12)
        react(last, slice(1, 2), 1)
        weigh(13)
        add_g(13, left_of(13))
        add_v(12)
        weigh(14)
        weigh(last, slice(0, 1))
        weigh(last, slice(1, 2), 1)
        store()
        add_v(14)
        finish(last, nc.vector, left_of(last), slice(0, 1))
        finish(last, nc.vector, left_of(last), slice(1, 2))
